import numpy as np, ml_dtypes
CORES = [113,118,241,246]
N = 4
BF = ml_dtypes.bfloat16
def gentries(a):
    return np.ascontiguousarray(a.reshape(8, 16, -1).transpose(0, 2, 1)).reshape(8, -1)
def gtable(e):
    e = np.asarray(e); return np.ascontiguousarray(e.reshape(8, -1, 16).transpose(0, 2, 1)).reshape(128, -1).astype(np.int32)
W, L, P, T = 4096, 192, 16, 7
def place(z, e, kap):
    return ((z * (2 * e + 1)[..., None] >> 5) + z + kap) & (W - 1)
def parts(rng):
    low = rng.random((N, 8, 1, W)) < rng.choice(np.array([0.01, 0.03, 0.06, 0.15, 0.5]), (N, 8, 1, 1))
    x = np.where(low, rng.integers(0, 256, (N, 8, 16, W)), rng.integers(64, 256, (N, 8, 16, W)))
    c = rng.integers(0, W, (N, 8, L, 16)); o = rng.integers(0, W, (N, 8, L, P))
    d = np.where(rng.random((N, 8, 1, L)) < 0.5, rng.integers(1, 49, (N, 8, 16, L)), rng.integers(1, 256, (N, 8, 16, L)))
    return x, c, o, d, rng.integers(0, 16, (N, 8, 16, 1))
def pack(x, c, o, d, w):
    return {"xt": np.ascontiguousarray(x.reshape(N, 128, W)).astype(np.float32).astype(BF), "pk": np.stack([gtable(a.reshape(8, -1)) for a in c]), "po": np.stack([gtable(a.reshape(8, -1)) for a in o]),
            "dm": np.ascontiguousarray(d.reshape(N, 128, L)).astype(np.int32), "wt": np.ascontiguousarray(w.reshape(N, 128, 1)).astype(np.int32)}
def setup_inputs(rng):
    return pack(*parts(rng))
def setup_inputs_ties(rng):
    x, c, o, d, w = parts(rng)
    v = rng.integers(8, 200, (N, 8, 16, 1))
    x = v + np.where(rng.random((N, 8, 1, W)) < 0.75, rng.integers(-1, 2, (N, 8, 1, W)), rng.integers(-1, 2, (N, 8, 16, W)))
    d = v + rng.integers(-1, 2, (N, 8, 16, L))
    few = rng.integers(0, W, 8); few[0] = 0; few[7] = W - 1
    c[:, 1::2] = few[rng.integers(0, 8, (N, 4, L, 16))]; o[:, 1::2] = few[rng.integers(0, 8, (N, 4, L, P))]
    return pack(x, c, o, d, w)
def setup_inputs_corners(rng):
    x, c, o, d, w = parts(rng)
    d = rng.choice(np.array([1, 2, 4, 5, 6, 8, 9, 10, 128, 246, 247, 248, 251, 252, 255]), (N, 8, 16, L))
    d[:, :, :, :8] = 1; d[:, :, :, L - 8:] = 255
    x[:, 0] = x[:, 0, :, :1]
    c[:, 1] = c[:, 1, :, :1]; o[:, 1] = o[:, 1, :, :1]
    o[:, 2] = np.concatenate([c[:, 2, :, ::-1]] * (P // 16), axis=2)
    w[:, 3] = 0; w[:, 4] = 15; w[:, 5] = 0; w[:, 5, 15] = rng.integers(1, 16, (N, 1))
    x[:, 6] = 255 * rng.integers(0, 2, (N, 1, W))
    x[:, 7] = rng.integers(0, 256, (N, 16, W)); c[:, 7] = (W - 1) * rng.integers(0, 2, (N, L, 16)); o[:, 7] = (W - 1) * rng.integers(0, 2, (N, L, P))
    q = int(rng.integers(0, N)); x[q] = x[q, :, :, :1]
    return pack(x, c, o, d, w)
def setup_inputs_ends(rng):
    kind = rng.integers(0, 4, (N, 8, 1, W)); hole = rng.integers(0, 16, (N, 8, 1, W))
    x = np.where(kind == 0, 0, np.where(kind == 1, 1, np.where(kind == 2, rng.integers(0, 2, (N, 8, 16, W)), np.arange(16).reshape(16, 1) != hole)))
    w = rng.integers(0, 2, (N, 8, 16, 1)); w[:, 6] = 0; w[:, 7] = 1; w = 15 * w
    kd = rng.integers(0, 4, (N, 8, 1, L)); d = np.where(kd == 0, 0, np.where(kd == 1, 1, rng.integers(0, 2, (N, 8, 16, L))))
    d[:, :, :, L - 1] = 1; d[:, :, :, L - 2] = 0; d = 1 + 254 * d
    c = (W - 1) * rng.integers(0, 2, (N, 8, L, 16)); o = (W - 1) * rng.integers(0, 2, (N, 8, L, P))
    c[:, :, L - 2:] = 0; c[:, :, L - 2:, 15] = W - 1; c[:, :, L - 1, 2] = W - 1
    o[:, :, L - 2:] = W - 1; o[:, :, L - 2:, P - 1] = 0; o[:, :, L - 1, 1] = 0
    c[0, :, :, 7] = W - 1; o[0, :, :, P - 1] = 0; c[0, 3, 5] = 0
    c[N - 1, :, :, 15] = W - 1; o[N - 1, :, :, P - 1] = 0
    m = rng.random((8, L, 1)) < 0.5; c[1] = np.where(m, 0, W - 1); o[1] = np.where(m, o[1], W - 1)
    e = np.add.reduce(w * d, axis=2) & 1023
    p = place(np.full((N, 8, L, 1), W - 1), e, 0)[..., 0]
    tail = int(np.argmax(place(np.arange(W)[None, :], np.zeros(1, np.int64), 0)[0]))
    for q in (0, 1, N - 1):
        for g in range(8): x[q, g][:, p[q, g]] = 1
        x[q, :, :, 0] = 0
    for q in (0, N - 1):
        c[q, 6, L - 2:, 15] = tail; x[q, 6, :, W - 1] = 1
    return pack(255 * x, c, o, d, w)
def setup_inputs_lull(rng):
    x, c, o, d, w = parts(rng)
    q = int(rng.integers(0, N)); p = (q - 1) % N
    x[q] = np.maximum(x[q], 1); x[:, :, :, :32] = 255; x[p, :, :, :32] = 0; x[q, :, :, :32] = 0
    c[p] = 0; o[q, :, :, P - 2:] = 0; o[q] = rng.permuted(o[q], axis=2)
    still = rng.permutation(8 * L)[:int(rng.integers(1, 32))]; c[q, still // L, still % L] = 0
    return pack(x, c, o, d, w)
def setup_inputs_spread(rng):
    x = np.minimum((np.exp2(8 * rng.random((N, 8, 1, W))) * (0.5 + 0.5 * rng.random((N, 8, 16, W)))).astype(np.int64), 255) * (rng.random((N, 8, 1, W)) > 0.0625)
    c = np.minimum((W * rng.random((N, 8, L, 16)) ** 4).astype(np.int64), W - 1); o = np.minimum((W * rng.random((N, 8, L, P)) ** 4).astype(np.int64), W - 1)
    d = np.minimum(np.maximum(np.exp2(8 * rng.random((N, 8, 16, L))).astype(np.int64), 1), 255)
    w = rng.integers(0, 16, (N, 8, 16, 1)) * (rng.random((N, 8, 16, 1)) < 0.4)
    return pack(x, c, o, d, w)
def check_inputs(d):
    bad = []
    for k, lo, hi in (("xt", 0, 255), ("pk", 0, W - 1), ("po", 0, W - 1), ("dm", 1, 255), ("wt", 0, 15)):
        v = np.asarray(d[k]).astype(np.float64)
        if not np.all((v >= lo) & (v <= hi) & (v == np.floor(v))): bad.append("range of " + k)
    return bad
def picks(x, z, e, kap):
    return np.take(x, place(z, e, kap) + (W * np.arange(8 * N)).reshape(N, 8, 1, 1), axis=0)
def reference(xt, pk, po, dm, wt):
    x = np.ascontiguousarray(xt.astype(np.float32).astype(np.int32).reshape(8 * N, 16, W).transpose(0, 2, 1)).reshape(-1, 16)
    c = np.stack([gentries(a) for a in pk]).astype(np.int64).reshape(N, 8, L, 16)
    o = np.stack([gentries(a) for a in po]).astype(np.int64).reshape(N, 8, L, P)
    D = np.ascontiguousarray(dm.astype(np.int32).reshape(N, 8, 16, L).transpose(0, 1, 3, 2))
    w = wt.astype(np.int32).reshape(N, 8, 1, 16)
    kap = np.zeros((N, 1, 1, 1), np.int64); left = []
    for t in range(T):
        if t > 0: c = np.roll(c, 1, axis=0)
        e = (np.add.reduce(w * D, axis=3) & 1023).astype(np.int64)
        a = picks(x, c, e, kap); b = picks(x, o, e, kap)
        if t >= N:
            m = left[t - N]; y = picks(x, m, e, kap); gone = (m != c)[..., None]
            up = np.max(np.where(gone, -1, a), axis=3) >= np.max(np.where(gone, y, -1), axis=3)
            D = np.minimum(np.maximum(np.where(up, D + 8, D - 8), 1), 255)
        sa = np.add.reduce(np.minimum(a, D[:, :, :, None, :]), axis=4); sb = np.add.reduce(np.minimum(b, D[:, :, :, None, :]), axis=4)
        k = np.argmax(sa, axis=3)[..., None]; j = np.argmin(sb, axis=3)[..., None]
        swap = np.take_along_axis(sa, k, 3) > np.take_along_axis(sb, j, 3)
        ck = np.take_along_axis(c, k, 3); oj = np.take_along_axis(o, j, 3)
        np.put_along_axis(c, k, np.where(swap, oj, ck), 3); np.put_along_axis(o, j, np.where(swap, ck, oj), 3)
        xk = np.take_along_axis(a, k[..., None], 3)[:, :, :, 0]
        D = np.where(swap & (xk >= D), np.maximum(D - 4, 1), D)
        kap = np.add.reduce(swap.reshape(N, -1).astype(np.int64), axis=1).reshape(N, 1, 1, 1) & 31
        left.append(c)
    return {"yc": np.stack([gtable(v.reshape(8, -1)) for v in c]).astype(np.float32), "yo": np.stack([gtable(v.reshape(8, -1)) for v in o]).astype(np.float32),
            "yd": np.ascontiguousarray(D.transpose(0, 1, 3, 2)).reshape(N, 128, L).astype(np.float32)}

@@ -1,0 +1,524 @@
+from concourse.bass import DstId, RemoteDMATransfer
+from concourse.mybir import AluOpType, AxisListType, ActivationFunctionType
+
+NV = 7
+A_ = AluOpType
+F_ = ActivationFunctionType
+TAB = 16
+WEND = TAB + 4096 + 32
+BIG = -100000.0
+VA, VDX = 2, 11
+
+
+def _sb(dtype, *names, w=192):
+    return {nm: ("sbuf", [128, w], dtype) for nm in names}
+
+
+SCRATCH = {"dx": ("sbuf", [128, 12, 256], "bfloat16"), "rrow": ("sbuf", [1, 128], "bfloat16"),
+           "c16": ("sbuf", [1, 192], "bfloat16"), "c3k": ("sbuf", [1, 16], "bfloat16"), "cff": ("sbuf", [1, 80], "bfloat16")}
+SCRATCH.update(_sb("bfloat16", "xtw", w=WEND))
+SCRATCH.update(_sb("bfloat16", "xo", "mo", "xc", "xa", "sa", w=3072))
+SCRATCH.update(_sb("bfloat16", "mc", w=3088))
+SCRATCH.update(_sb("bfloat16", "E", "NE", "WE", w=2048))
+SCRATCH.update(_sb("bfloat16", "idn", "nid", "id4", "id16", "neg", w=128))
+SCRATCH.update(_sb("bfloat16", "bd8", w=8))
+SCRATCH.update(_sb("bfloat16", "ones", "rst", "D0", "D1", "D2", "Dt", "gn", "ind", "yb0", "yb1", "yb2", "up"))
+SCRATCH.update(_sb("int32", "pki", "poi", "dmi", "pi", "pf", "ci", "cf", "mi", "mf", "sO"))
+SCRATCH.update(_sb("uint16", "offo", "offc", "offa"))
+SCRATCH.update(_sb("float32", "O0", "O1", "am", "kO", "kC", "OHO", "wO", "so", "Q", "sP", "OHP", "ds", "OO",
+                   "ydf", "ycf", "yof"))
+SCRATCH.update(_sb("float32", "cv1", "cv2", "cv3", "cv4", w=384))
+SCRATCH.update(_sb("int32", "wti", "kq", w=1))
+SCRATCH.update(_sb("float32", "wtf", "K", "kc", w=1))
+SCRATCH.update(_sb("int32", "iP", "iC", "irow", "igp", "ich", "it0", "it1", "it2", "it3", "it4", w=24))
+SCRATCH.update(_sb("uint16", "dupi", "dupo", w=24))
+SCRATCH.update(_sb("uint16", "pick", "picko", "rep", "rep15", "aoff", w=12))
+SCRATCH.update(_sb("int32", "ei", "eu", "hiO", "eff", "lo", w=16))
+SCRATCH.update(_sb("float32", "vp", "thr", w=16))
+SCRATCH.update(_sb("uint16", "offs", w=16))
+SCRATCH.update(_sb("bfloat16", "sw", w=16))
+SCRATCH.update(_sb("float32", "nn", w=72))
+SCRATCH.update(_sb("float32", "ev", "evs", "ym", w=36))
+SCRATCH.update(_sb("int32", "yq", "yf", w=36))
+SCRATCH.update(_sb("uint16", "yoff", w=36))
+SCRATCH.update(_sb("float32", "cin", "cout", w=192 * NV))
+SCRATCH.update(_sb("float32", "rec", w=24 * (NV - 1)))
+SCRATCH.update(_sb("float32", "rin", w=72 * NV))
+PSUM = ("pd0", "pd1", "pkO", "pkA", "pkB", "pM1", "pM2", "pZ")
+SCRATCH.update({nm: ("psum", [128, 512], "float32") for nm in PSUM})
+SEMAPHORES = (["sv", "ss", "sp", "sg", "ls", "l_po", "l_dm", "l_pk", "l_wt", "l_xt", "s_yc", "s_yo", "s_yd"]
+              + ["arr%d" % t for t in range(1, NV)] + [nm + str(t) for t in range(4, NV) for nm in ("ra", "rb")])
+
+
+def rank_program(g, core, T, topo):
+    rank = T.rank_of(core)
+    if rank is None:
+        return
+    n = len(T.cores)
+    queue = {"v": g.vector, "s": g.scalar, "p": g.tensor, "g": g, "y": g.sync}
+    own = {"v": "sv", "s": "ss", "p": "sp", "g": "sg"}
+    count = {"sv": 0, "ss": 0, "sp": 0, "sg": 0}
+    known = {q: {} for q in queue}
+    snap = {}
+    last_w, readers = {}, {}
+
+    def need(q, sem, val):
+        if known[q].get(sem, 0) >= val:
+            return
+        queue[q].wait_ge(T.sem[sem], val)
+        known[q][sem] = val
+        for k2, v2 in snap.get((sem, val), {}).items():
+            if known[q].get(k2, 0) < v2:
+                known[q][k2] = v2
+
+    def order(q, reads, writes):
+        deps = {}
+
+        def add(tok, skip_own=False):
+            for sm, c in tok.items():
+                if skip_own and sm == own.get(q):
+                    continue
+                if deps.get(sm, 0) < c:
+                    deps[sm] = c
+        for b in reads:
+            add(last_w.get(b, {}))
+            if b in PSUM:
+                add(readers.get(b, {}), True)
+        for b in writes:
+            add(last_w.get(b, {}), q == "p")
+            add(readers.get(b, {}), True)
+        for sm in sorted(deps):
+            need(q, sm, deps[sm])
+
+    def note(tok_sem, tok_val, reads, writes):
+        for b in writes:
+            last_w[b] = {tok_sem: tok_val}
+            readers[b] = {}
+        for b in reads:
+            readers.setdefault(b, {})[tok_sem] = tok_val
+
+    def op(q, fn, reads, writes):
+        order(q, reads, writes)
+        sem = own[q]
+        fn().then_inc(T.sem[sem], 1)
+        count[sem] += 1
+        snap[(sem, count[sem])] = dict(known[q])
+        note(sem, count[sem], reads, writes)
+
+    def dma(q, out, in_, sem, reads, writes):
+        order(q, reads, writes)
+        queue[q].dma_start(out, in_).then_inc(T.sem[sem], 16)
+        snap[(sem, 16)] = dict(known[q])
+        note(sem, 16, reads, writes)
+
+    def arrived(buf, sem, val):
+        last_w[buf] = {sem: val}
+        readers[buf] = {}
+
+    v, s, pe = g.vector, g.scalar, g.tensor
+    width = {"cin": 192, "cout": 192, "rec": 24, "rin": 72}
+
+    def X(name):
+        base = name.rstrip("0123456789")
+        if base not in width:
+            return T[name][:]
+        w = width[base]
+        i = int(name[len(base):])
+        return T[base][:, w * i:w * i + w]
+
+    def V(fn, r, w):
+        op("v", fn, r, w)
+
+    def copy_s(out, in_, r, w, f=F_.Copy):
+        op("s", lambda: s.activation(out, in_, f), r, w)
+
+    def copy_v(out, in_, r, w):
+        V(lambda: v.tensor_copy(out, in_), r, w)
+
+    def fill(ap, c, w):
+        V(lambda: v.memset(ap, c), [], w)
+
+    def tt(out, a, b, o, r, w):
+        V(lambda: v.tensor_tensor(out, a, b, o), r, w)
+
+    def ts(out, a, s1, o0, r, w):
+        V(lambda: v.tensor_scalar(out, a, s1, None, o0), r, w)
+
+    def ts2(out, a, s1, s2, o0, o1, r, w):
+        V(lambda: v.tensor_scalar(out, a, s1, s2, o0, o1), r, w)
+
+    def scan(out, d0, d1, o1, r, w):
+        V(lambda: v.tensor_tensor_scan(out, d0, d1, 0.0, A_.mult, o1), r, w)
+
+    def mm(out, lhsT, rhs, st, sp, r, w):
+        op("p", lambda: pe.matmul(out, lhsT, rhs, st, sp), r, w)
+
+    def blk(nm, c0, c1):
+        return ["%s%d" % (nm, c) for c in range(c0, c1)]
+
+    dma("y", T.dmi[:], T.dm[:], "l_dm", [], ["dmi"])
+    dma("y", T.poi[:], T.po[:], "l_po", [], ["poi"])
+    dma("y", T.wti[:], T.wt[:], "l_wt", [], ["wti"])
+    dma("s", T.xtw[:, TAB:TAB + 4096], T.xt[:], "l_xt", [], ["xtw"])
+    dma("y", T.pki[:], T.pk[:], "l_pk", [], ["pki"])
+    fill(T.bd8[:], 4096.0, ["bd8"])
+    fill(T.ones[:], 1.0, ["ones"])
+    fill(T.E[:], 0.0, ["E"])
+    op("g", lambda: g.affine_select(T.bd8[:], T.bd8[:], [[-16, 8]], A_.is_ge, 0.0, 0, 1), ["bd8"], ["bd8"])
+    op("g", lambda: g.affine_select(T.bd8[:], T.bd8[:], [[16, 8]], A_.is_ge, 0.0, 15, -1), ["bd8"], ["bd8"])
+    op("g", lambda: g.iota(T.iP[:], [[0, 24]], 0, 1), [], ["iP"])
+    op("g", lambda: g.iota(T.iC[:], [[1, 24]], 0, 0), [], ["iC"])
+    op("g", lambda: g.affine_select(T.idn[:], T.ones[:, 0:128], [[-1, 128]], A_.is_equal, 0.0, 0, 1), ["ones"], ["idn"])
+    op("g", lambda: g.iota(T.rrow[:], [[0, 8], [1, 16]], 0, 0, allow_small_or_imprecise_dtypes=True), [], ["rrow"])
+    op("g", lambda: g.iota(T.c16[:], [[16, 192]], 0, 0, allow_small_or_imprecise_dtypes=True), [], ["c16"])
+    for r in range(16):
+        copy_s(T.E[:, r * 129:(r + 1) * 128:16], T.bd8[:], ["bd8", "E"], ["E%d" % r])
+    EA = ["E"] + blk("E", 0, 16)
+    ts(T.irow[:], T.iP[:], 15, A_.bitwise_and, ["iP"], ["irow"])
+    ts(T.ich[:], T.iC[:], 1, A_.logical_shift_right, ["iC"], ["ich"])
+    ts2(T.igp[:], T.iP[:], 4, 1, A_.logical_shift_right, A_.bitwise_and, ["iP"], ["igp"])
+    ts(T.it0[:], T.ich[:], 16, A_.mult, ["ich"], ["it0"])
+    copy_v(T.D0[:], T.dmi[:], ["dmi"], ["D0"])
+    tt(T.it1[:], T.it0[:], T.irow[:], A_.add, ["it0", "irow"], ["it1"])
+    ts(T.igp[:], T.igp[:], 16, A_.mult, ["igp"], ["igp"])
+    copy_v(T.dupi[:], T.it1[:], ["it1"], ["dupi"])
+    ts2(T.it2[:, 0:12], T.iC[:, 0:12], 32, 15, A_.mult, A_.add, ["iC"], ["it2"])
+    tt(T.it3[:, 0:12], T.igp[:, 0:12], T.irow[:, 0:12], A_.subtract, ["igp", "irow"], ["it3"])
+    copy_v(T.rep[:], T.iC[:, 0:12], ["iC"], ["rep"])
+    tt(T.it2[:, 0:12], T.it2[:, 0:12], T.it3[:, 0:12], A_.add, ["it2", "it3"], ["it2"])
+    ts(T.wtf[:], T.wti[:], 1.0 / 2048, A_.mult, ["wti"], ["wtf"])
+    copy_v(T.pick[:], T.it2[:, 0:12], ["it2"], ["pick"])
+
+    def seat_in(src, dst, a, b):
+        copy_v(T[a][:], T[src][:].indirect(T.dupi[:]), [src, "dupi"], [a])
+        V(lambda: v.transpose(T[b][:], T[a][:]), [a], [b])
+        copy_v(X(dst), T[b][:].indirect(T.pick[:]), [b, "pick"], [dst])
+
+    def seat_out(src, dst, a, b, out, sem, q, cp):
+        cp(T[a][:], X(src).indirect(T.dupo[:]), [src, "dupo"], [a])
+        V(lambda: v.transpose(T[b][:], T[a][:]), [a], [b])
+        cp(T[dst][:], T[b][:].indirect(T.picko[:]), [b, "picko"], [dst])
+        dma(q, out[:], T[dst][:], sem, [dst], [])
+
+    seat_in("poi", "O0", "cv1", "cv2")
+    ts(T.WE[:], T.E[:], T.wtf[:, 0:1], A_.mult, EA + ["wtf"], ["WE"])
+    fill(T.K[:], 0.0, ["K"])
+    ts(T.nid[:], T.idn[:], -1.0, A_.mult, ["idn"], ["nid"])
+    fill(T.c3k[:], 3072.0, ["c3k"])
+    fill(T.cff[:], 4096.0 * 4080, ["cff"])
+    fill(T.cff[:, 68:72], 0.0, ["cff"])
+
+    def constants_1():
+        ts(T.NE[:], T.E[:], -1.0, A_.mult, EA, ["NE"])
+        fill(T.mc[:, 3072:3088], 512.0, ["mc_end"])
+        fill(T.Dt[:, 128:192], 0.0, ["Dt0"])
+        ts(T.id4[:], T.idn[:], -4.0, A_.mult, ["idn"], ["id4"])
+        fill(T.rst[:], 1.0, ["rst"])
+        fill(T.rst[:, 0:192:16], 0.0, ["rst"])
+        ts2(T.it4[:, 0:12], T.iC[:, 0:12], 16, 15, A_.mult, A_.add, ["iC"], ["it4"])
+        copy_v(T.rep15[:], T.it4[:, 0:12], ["it4"], ["rep15"])
+
+    def constants_2():
+        fill(T.xtw[:, 0:TAB], -1.0, ["xt_m1"])
+        fill(T.neg[:], -0.0625, ["neg"])
+        ts(T.id16[:], T.idn[:], 16.0, A_.mult, ["idn"], ["id16"])
+        ts2(T.it2[:, 0:12], T.iC[:, 0:12], 256, 240, A_.mult, A_.add, ["iC"], ["it2"])
+        tt(T.it2[:, 0:12], T.it2[:, 0:12], T.irow[:, 0:12], A_.add, ["it2", "irow"], ["it2"])
+        copy_v(T.aoff[:], T.it2[:, 0:12], ["it2"], ["aoff"])
+
+    def constants_3():
+        ts(T.it1[:], T.it0[:], 15, A_.add, ["it0"], ["it1"])
+        tt(T.it1[:], T.it1[:], T.irow[:], A_.subtract, ["it1", "irow"], ["it1"])
+        copy_v(T.dupo[:], T.it1[:], ["it1"], ["dupo"])
+        ts(T.it4[:, 0:12], T.iC[:, 0:12], 32, A_.mult, ["iC"], ["it4"])
+        tt(T.it4[:, 0:12], T.it4[:, 0:12], T.irow[:, 0:12], A_.add, ["it4", "irow"], ["it4"])
+        tt(T.it4[:, 0:12], T.it4[:, 0:12], T.igp[:, 0:12], A_.add, ["it4", "igp"], ["it4"])
+        copy_v(T.picko[:], T.it4[:, 0:12], ["it4"], ["picko"])
+
+    win = T.xtw[:, TAB:WEND]
+    winm = T.xtw[:, 0:WEND]
+    XT = ["xtw", "xt_wrap"]
+    XTM = ["xtw", "xt_wrap", "xt_m1"]
+    DX = blk("dx", 0, 16)
+
+    def E(r):
+        return T.E[:, r * 128:(r + 1) * 128]
+
+    def emit_e(dn):
+        for r in range(16):
+            mm(T.pM2[:, 0:12], T.WE[:, r * 128:(r + 1) * 128], T[dn][:, r:192:16], r == 0, r == 15, ["WE", dn], ["pM2"])
+
+    def emit_v():
+        copy_v(T.ei[:, 0:12], T.pM2[:, 0:12], ["pM2"], ["ei"])
+        ts(T.eu[:, 0:12], T.ei[:, 0:12], 2047, A_.bitwise_and, ["ei"], ["eu"])
+        ts(T.vp[:, 0:12], T.eu[:, 0:12], 33.0, A_.add, ["eu"], ["vp"])
+
+    def columns(cards, a, b):
+        tt(T[a][:], T.vp[:, 0:12].indirect(T.rep[:]), X(cards), A_.mult, ["vp", "rep", cards], [a])
+        ts2(T[b][:], T[a][:], 5, 4095, A_.arith_shift_right, A_.bitwise_and, [a], [b])
+
+    def emit_list(cards, a, b, off):
+        columns(cards, a, b)
+        ts(T[off][:], T[b][:], T.K[:, 0:1], A_.add, [b, "K"], [off])
+
+    def emit_dx(dn, onv):
+        for k in range(16):
+            (copy_v if k in onv else copy_s)(T.dx[:, :, 16 * k:16 * k + 16], T[dn][:], [dn], ["dx%d" % k])
+
+    def emit_sd(dn):
+        mm(T.pkO[:, 192:204], T.ones[0:1, 0:128], T.c3k[0:1, 0:12], True, False, ["ones", "c3k"], ["pkO"])
+        mm(T.pkO[:, 192:204], T.ones[0:1, 0:128], T.cff[0:1, 64:76], False, False, ["ones", "cff"], ["pkO"])
+        for r in range(16):
+            mm(T.pkO[:, 196:200], E(r), T[dn][:, 64 + r:128:16], False, r == 15, ["E%d" % r, dn], ["pkO"])
+
+    def gather(onv, dst, off, c0, c1, w=None):
+        o = T[dst][:, 256 * c0:256 * c1]
+        i = (w or win).indirect(T[off][:, 16 * c0:16 * c1])
+        (copy_v if onv else copy_s)(o, i, (XTM if w is not None else XT) + [off], blk(dst, c0, c1))
+
+    def fused(dst, off, c0, c1):
+        for c in range(c0, c1):
+            tt(T[dst][:, 256 * c:256 * c + 256], win.indirect(T[off][:, 16 * c:16 * c + 16]), T.dx[:, c, :], A_.min,
+               XT + [off] + DX, ["%s%d" % (dst, c)])
+
+    def minus_x(j, src):
+        b = "pd%d" % (j % 2)
+        mm(T[b][:], T.nid[:], T[src][:, 512 * j:512 * j + 512], True, False, ["nid"] + blk(src, 2 * j, 2 * j + 2), [b])
+
+    def plus_d(j, dst):
+        b = "pd%d" % (j % 2)
+        mm(T[b][:, 0:256], T.idn[:], T.dx[:, 2 * j, :], False, False, ["idn"] + DX, [b])
+        mm(T[b][:, 256:512], T.idn[:], T.dx[:, 2 * j + 1, :], False, True, ["idn"] + DX, [b])
+        copy_s(T[dst][:, 512 * j:512 * j + 512], T[b][:], [b], blk(dst, 2 * j, 2 * j + 2), F_.Relu)
+
+    def pair(j, src, dst):
+        minus_x(j, src)
+        plus_d(j, dst)
+
+    def bias(bank, lo, hi, ff):
+        mm(T[bank][:, 0:hi - lo], T.ones[0:1, 0:128], T.c16[0:1, lo:hi], True, False, ["ones", "c16"], [bank])
+        mm(T[bank][:, 0:hi - lo], T.rrow[0:1, :], T.ones[0:1, 0:hi - lo], False, False, ["ones", "rrow"], [bank])
+        if ff:
+            mm(T[bank][:, 0:ff], T.ones[0:1, 0:128], T.cff[0:1, 0:ff], False, False, ["ones", "cff"], [bank])
+
+    def score(bank, src, c0, at, neg, final):
+        for r in range(16):
+            mm(T[bank][:, at:at + 64], T.NE[:, r * 128:(r + 1) * 128] if neg else E(r),
+               T[src][:, 256 * c0 + r:256 * c0 + 1024:16], False, final and r == 15,
+               ["NE" if neg else "E%d" % r] + blk(src, c0, c0 + 4), [bank])
+
+    def send_pack(t):
+        dst = T.cores[(rank + 1) % n]
+        rid, pid = topo.addr(dst, core)
+        need("g", *list(last_w["cout%d" % t].items())[0])
+        eng = topo.engines(core, dst)[:8]
+        g.remote_dma(X("cin%d" % (t + 1)), X("cout%d" % t), T.sem["arr%d" % (t + 1)], T.sem.ls, pid, rid,
+                     sum(1 << e for e in eng))
+        return len(eng)
+
+    def send_rec(q):
+        need("g", *list(last_w["rec%d" % q].items())[0])
+        trs = []
+        for d in (1, 2, 3):
+            t = q + d
+            if t < 4 or t >= NV:
+                continue
+            dst = T.cores[(rank + d) % n]
+            rid, pid = topo.addr(dst, core)
+            eng = topo.engines(core, dst)[2 * len(trs):2 * len(trs) + 2]
+            b = 72 * t + 24 * (q - (t - 3))
+            trs.append(RemoteDMATransfer(dst_ids=[DstId(rid=rid, pnc=pid)], dma_engine_mask=sum(1 << e for e in eng),
+                                         remote_sem=T.sem[("rb%d" if d == 1 else "ra%d") % t], srcs=[X("rec%d" % q)],
+                                         dsts=[T.rin[:, b:b + 24]]))
+        if trs:
+            g.remote_dma_fused(trs, local_sem=T.sem.ls)
+        return 2 * len(trs)
+
+    left = 0
+    dcur, ocur = "D0", "O0"
+    emit_e("D0")
+    emit_v()
+    emit_dx("D0", ())
+    copy_s(T.xtw[:, TAB + 4096:WEND], T.xtw[:, TAB:TAB + 32], ["xtw"], ["xt_wrap"])
+    for t in range(NV):
+        back = t >= 4
+        last = t == NV - 1
+        c_in, c_out, mback = "cin%d" % t, "cout%d" % t, "cout%d" % (t - 4)
+        onx = "O1" if t % 2 == 0 else "O0"
+        emit_list(ocur, "pi", "pf", "offo")
+        gather(False, "xo", "offo", 4, 6)
+        copy_s(T.pZ[:, 0:192], X(ocur), [ocur], ["pZ"])
+        if back:
+            copy_s(T.pZ[:, 192:384], X(mback), [mback], ["pZ"])
+        gather(False, "xo", "offo", 6, 8)
+        if not back:
+            emit_sd(dcur)
+            pair(2, "xo", "mo")
+            if t == 0:
+                constants_1()
+                seat_in("pki", "cin0", "cv3", "cv4")
+            fused("mo", "offo", 0, 4)
+            gather(False, "xo", "offo", 8, 10)
+            pair(3, "xo", "mo")
+            gather(False, "xo", "offo", 10, 12)
+            if t == 1:
+                constants_2()
+            if t == 2:
+                constants_3()
+            if t > 0:
+                arrived(c_in, "arr%d" % t, 8)
+            emit_list(c_in, "ci", "cf", "offc")
+            bias("pkO", 0, 192, 64)
+            score("pkO", "mo", 0, 0, True, False)
+            pair(4, "xo", "mo")
+            score("pkO", "mo", 4, 64, False, False)
+            pair(5, "xo", "mo")
+            gather(False, "xc", "offc", 8, 10)
+            fused("mc", "offc", 0, 4)
+            bias("pkA", 0, 128, 0)
+            score("pkA", "mc", 0, 0, False, False)
+            score("pkO", "mo", 8, 128, False, True)
+            gather(False, "xc", "offc", 10, 12)
+            copy_s(T.kO[:], T.pkO[:, 0:192], ["pkO"], ["kO"])
+            pair(4, "xc", "mc")
+            fused("mc", "offc", 4, 8)
+            pair(5, "xc", "mc")
+        else:
+            gather(False, "xo", "offo", 8, 12)
+            P = [T.rin[:, 72 * t + 24 * i:72 * t + 24 * i + 12] for i in range(3)]
+            C = [T.rin[:, 72 * t + 24 * i + 12:72 * t + 24 * i + 24] for i in range(3)]
+            arrived("old", "ra%d" % t, 4)
+            arrived("new", "rb%d" % t, 2)
+            arrived(c_in, "arr%d" % t, 8)
+
+            def first(i, r):
+                tt(T.yq[:, 12 * i:12 * i + 12], T.vp[:, 0:12], C[i], A_.mult, ["vp", r], ["yq%d" % i])
+            columns(mback, "mi", "mf")
+            ts2(T.nn[:, 0:48], T.rin[:, 72 * t:72 * t + 48], 3072.0, BIG, A_.is_ge, A_.mult, ["old"], ["nna"])
+            tt(T.ev[:, 0:12], P[0], P[1], A_.is_equal, ["old"], ["ev0"])
+            first(0, "old")
+            first(1, "old")
+            tt(T.gn[:], X(c_in), T.pZ[:, 192:384], A_.not_equal, [c_in, "pZ"], ["gn"])
+            ts(T.pM2[:, 128:320], T.gn[:], BIG, A_.mult, ["gn"], ["pM2"])
+            tt(T.am[:], T.mf[:], T.pM2[:, 128:320], A_.add, ["mf", "pM2"], ["am"])
+            ts2(T.offa[:], T.am[:], T.K[:, 0:1], float(TAB), A_.add, A_.add, ["am", "K"], ["offa"])
+            va = 12 - VA
+            for c in range(0, va, 3):
+                gather(False, "xa", "offa", c, min(c + 3, va), winm)
+            emit_list(c_in, "ci", "cf", "offc")
+            ts2(T.nn[:, 48:72], T.rin[:, 72 * t + 48:72 * t + 72], 3072.0, BIG, A_.is_ge, A_.mult, ["new"], ["nnb"])
+            tt(T.ev[:, 12:24], P[0], P[2], A_.is_equal, ["old", "new"], ["ev1"])
+            tt(T.ev[:, 24:36], P[1], P[2], A_.is_equal, ["old", "new"], ["ev2"])
+            first(2, "new")
+            ts(T.evs[:], T.ev[:], BIG, A_.mult, blk("ev", 0, 3), ["evs"])
+            ts2(T.yf[:], T.yq[:], 5, 4095, A_.arith_shift_right, A_.bitwise_and, blk("yq", 0, 3), ["yf"])
+            for i in range(3):
+                tt(T.ym[:, 12 * i:12 * i + 12], T.yf[:, 12 * i:12 * i + 12], T.nn[:, 24 * i:24 * i + 12], A_.add,
+                   ["yf", "nna" if i < 2 else "nnb"], ["ym%d" % i])
+            tt(T.ym[:, 12:36], T.ym[:, 12:36], T.evs[:, 0:24], A_.add, ["ym1", "ym2", "evs"], ["ym1", "ym2"])
+            tt(T.ym[:, 24:36], T.ym[:, 24:36], T.evs[:, 24:36], A_.add, ["ym2", "evs"], ["ym2"])
+            ts2(T.yoff[:], T.ym[:], T.K[:, 0:1], float(TAB), A_.add, A_.add, blk("ym", 0, 3) + ["K"], ["yoff"])
+            if VA:
+                gather(True, "xa", "offa", va, 12, winm)
+            copy_v(T.yb0[:], winm.indirect(T.yoff[:, 0:12]), XTM + ["yoff"], ["yb0"])
+            tt(T.yb1[:], winm.indirect(T.yoff[:, 12:24]), T.yb0[:], A_.max, XTM + ["yoff", "yb0"], ["yb1"])
+            tt(T.yb2[:], winm.indirect(T.yoff[:, 24:36]), T.yb1[:], A_.max, XTM + ["yoff", "yb1"], ["yb2"])
+            gather(False, "xc", "offc", 8, 12)
+            mm(T.pM1[:, 0:192], T.neg[:], T.ones[:], True, False, ["neg", "ones"], ["pM1"])
+            mm(T.pM1[:, 0:192], T.idn[:], T[dcur][:], False, False, ["idn", dcur], ["pM1"])
+            minus_x(2, "xo")
+            minus_x(3, "xo")
+            for r in range(16):
+                scan(T.sa[:, r:3072:16], T.rst[:], T.xa[:, r:3072:16], A_.max, ["rst"] + blk("xa", 0, 12), ["sa%d" % r])
+            tt(T.up[:], T.sa[:].indirect(T.aoff[:]), T.yb2[:], A_.is_ge, blk("sa", 0, 16) + ["aoff", "yb2"], ["up"])
+            mm(T.pM1[:, 0:192], T.id16[:], T.up[:], False, True, ["id16", "up"], ["pM1"])
+            ts2(T.D2[:], T.pM1[:, 0:192], 1.0, 255.0, A_.max, A_.min, ["pM1"], ["D2"])
+            dcur = "D2"
+            emit_sd(dcur)
+            emit_dx(dcur, range(VDX))
+            fused("mo", "offo", 0, 4)
+            plus_d(2, "mo")
+            plus_d(3, "mo")
+            pair(4, "xo", "mo")
+            bias("pkO", 0, 192, 64)
+            score("pkO", "mo", 0, 0, True, False)
+            pair(5, "xo", "mo")
+            pair(4, "xc", "mc")
+            score("pkO", "mo", 4, 64, False, False)
+            fused("mc", "offc", 0, 4)
+            score("pkO", "mo", 8, 128, False, True)
+            pair(5, "xc", "mc")
+            copy_s(T.kO[:], T.pkO[:, 0:192], ["pkO"], ["kO"])
+            bias("pkA", 0, 128, 0)
+            score("pkA", "mc", 0, 0, False, False)
+            fused("mc", "offc", 4, 8)
+        score("pkA", "mc", 4, 64, False, True)
+        copy_s(T.kC[:, 0:128], T.pkA[:, 0:128], ["pkA"], ["kCa"])
+        copy_s(T.Dt[:, 0:128], T[dcur][:, 0:128], [dcur], ["Dt"])
+        bias("pkB", 128, 192, 64)
+        score("pkB", "mc", 8, 0, True, True)
+        mm(T.pM1[:, 0:192], T.idn[:], T[dcur][:], True, False, ["idn", dcur], ["pM1"])
+        scan(T.sO[:], T.rst[:], T.kO[:], A_.max, ["rst", "kO"], ["sO"])
+        ts(T.hiO[:, 0:12], T.sO[:, 15:192:16], 0xFFF000, A_.bitwise_and, ["sO"], ["hiO"])
+        tt(T.OHO[:], T.sO[:].indirect(T.rep15[:]), T.kO[:], A_.is_equal, ["sO", "rep15", "kO"], ["OHO"])
+        tt(T.thr[:, 0:12], T.pkO[:, 192:204], T.hiO[:, 0:12], A_.subtract, ["pkO", "hiO"], ["thr"])
+        tt(T.wO[:], T.OHO[:], T.pZ[:, 0:192], A_.mult, ["OHO", "pZ"], ["wO"])
+        scan(T.so[:], T.rst[:], T.wO[:], A_.add, ["rst", "wO"], ["so"])
+        tt(T.Q[:], T.so[:].indirect(T.rep15[:]), X(c_in), A_.subtract, ["so", "rep15", c_in], ["Q"])
+        copy_s(T.pZ[:, 192:384], T.Q[:], ["Q"], ["pZ"])
+        scan(T.sP[:, 0:128], T.rst[:, 0:128], T.kC[:, 0:128], A_.max, ["rst", "kCa"], ["sPa"])
+        scan(T.sP[:, 128:192], T.rst[:, 128:192], T.pkB[:, 0:64], A_.max, ["rst", "pkB"], ["sPb"])
+        copy_s(T.kC[:, 128:192], T.pkB[:, 0:64], ["pkB"], ["kCb"])
+        tt(T.eff[:, 0:12], T.sP[:, 15:192:16], T.thr[:, 0:12], A_.max, ["sPa", "sPb", "thr"], ["eff"])
+        ts(T.lo[:, 0:12], T.eff[:, 0:12], 4095, A_.bitwise_and, ["eff"], ["lo"])
+        if not last:
+            tt(T.sw[:, 0:12], T.eff[:, 0:12], T.thr[:, 0:12], A_.is_gt, ["eff", "thr"], ["sw"])
+            mm(T.pM2[:, 16:28], T.ones[:, 0:128], T.sw[:, 0:12], True, True, ["ones", "sw"], ["pM2"])
+        copy_v(T.offs[:, 0:12], T.lo[:, 0:12], ["lo"], ["offs"])
+        tt(T.ind[:], T.mc[:].indirect(T.offs[:, 0:12]), T.Dt[:], A_.is_equal,
+           blk("mc", 0, 12) + ["mc_end", "offs", "Dt", "Dt0"], ["ind"])
+        mm(T.pM1[:, 0:192], T.id4[:], T.ind[:], False, True, ["id4", "ind"], ["pM1"])
+        tt(T.OHP[:], T.eff[:, 0:12].indirect(T.rep[:]), T.kC[:], A_.is_equal, ["eff", "rep", "kCa", "kCb"], ["OHP"])
+
+        def pack_out():
+            tt(T.pkA[:, 192:384], T.OHP[:], T.pZ[:, 192:384], A_.mult, ["OHP", "pZ"], ["pkA"])
+            tt(X(c_out), X(c_in), T.pkA[:, 192:384], A_.add, [c_in, "pkA"], [c_out])
+            return 0 if last else send_pack(t)
+        if t >= 3:
+            left += pack_out()
+        if last:
+            ts(T.ydf[:], T.pM1[:, 0:192], 1.0, A_.max, ["pM1"], ["ydf"])
+            dma("y", T.yd[:], T.ydf[:], "s_yd", ["ydf"], [])
+        else:
+            nxt = "D1" if t % 2 == 0 else "D0"
+            ts(T[nxt][:], T.pM1[:, 0:192], 1.0, A_.max, ["pM1"], [nxt])
+            dcur = nxt
+            V(lambda: v.tensor_reduce(T.kc[:], T.pM2[:, 16:28], AxisListType.X, A_.add), ["pM2"], ["kc"])
+            emit_e(dcur)
+            if t + 1 < 4:
+                emit_dx(dcur, ())
+        if t < 3:
+            left += pack_out()
+        scan(T.ds[:], T.rst[:], T.pkA[:, 192:384], A_.add, ["rst", "pkA"], ["ds"])
+        if not last:
+            ts2(T.kq[:], T.kc[:], 1.0 / 32, -0.5 + 1.0 / 64, A_.mult, A_.add, ["kc"], ["kq"])
+        tt(T.OO[:], T.ds[:].indirect(T.rep15[:]), T.OHO[:], A_.mult, ["ds", "rep15", "OHO"], ["OO"])
+        if not last:
+            ts2(T.K[:], T.kq[:], -32.0, T.kc[:, 0:1], A_.mult, A_.add, ["kq", "kc"], ["K"])
+        tt(X(onx), T.pZ[:, 0:192], T.OO[:], A_.subtract, ["pZ", "OO"], [onx])
+        if not last:
+            emit_v()
+        if last:
+            seat_out(c_out, "ycf", "cv1", "cv2", T.yc, "s_yc", "y", copy_s)
+            seat_out(onx, "yof", "cv3", "cv4", T.yo, "s_yo", "y", copy_v)
+        if 1 <= t < NV - 1:
+            rc = "rec%d" % t
+            copy_v(T.rec[:, 24 * t:24 * t + 12], T.lo[:, 0:12], ["lo"], [rc])
+            tt(T.rec[:, 24 * t + 12:24 * t + 24], T.so[:, 15:192:16], T.ds[:, 15:192:16], A_.subtract, ["so", "ds"], [rc])
+            left += send_rec(t)
+        ocur = onx
+    for sem in ("sv", "ss", "sp", "sg"):
+        need("g", sem, count[sem])
+    for sem in ("l_po", "l_dm", "l_pk", "l_wt", "l_xt", "s_yc", "s_yo", "s_yd"):
+        need("g", sem, 16)
+    g.wait_ge(T.sem.ls, left)

@@ -4,50 +4,53 @@ from concourse.mybir import AluOpType, AxisListType, ActivationFunctionType
 NV = 7
 A_ = AluOpType
 F_ = ActivationFunctionType
-TAB = 16
-WEND = TAB + 4096 + 32
-BIG = -100000.0
-VA, VDX = 2, 11
+WT = 4096 + 32
+RN = 10
+RP, RC = 7, 11
+VA = 80
+CUTN, CUTR = (4, 7, 3, 5, 8), (4, 4, 6, 9)
+KS, KG = 9, 0
+XE, XF = 144, 168
+KR = 5
+ZB = 129 * 2048
 
 
 def _sb(dtype, *names, w=192):
     return {nm: ("sbuf", [128, w], dtype) for nm in names}
 
 
-SCRATCH = {"dx": ("sbuf", [128, 12, 256], "bfloat16"), "rrow": ("sbuf", [1, 128], "bfloat16"),
-           "c16": ("sbuf", [1, 192], "bfloat16"), "c3k": ("sbuf", [1, 16], "bfloat16"), "cff": ("sbuf", [1, 80], "bfloat16")}
-SCRATCH.update(_sb("bfloat16", "xtw", w=WEND))
-SCRATCH.update(_sb("bfloat16", "xo", "mo", "xc", "xa", "sa", w=3072))
-SCRATCH.update(_sb("bfloat16", "mc", w=3088))
-SCRATCH.update(_sb("bfloat16", "E", "NE", "WE", w=2048))
-SCRATCH.update(_sb("bfloat16", "idn", "nid", "id4", "id16", "neg", w=128))
-SCRATCH.update(_sb("bfloat16", "bd8", w=8))
-SCRATCH.update(_sb("bfloat16", "ones", "rst", "D0", "D1", "D2", "Dt", "gn", "ind", "yb0", "yb1", "yb2", "up"))
-SCRATCH.update(_sb("int32", "pki", "poi", "dmi", "pi", "pf", "ci", "cf", "mi", "mf", "sO"))
-SCRATCH.update(_sb("uint16", "offo", "offc", "offa"))
-SCRATCH.update(_sb("float32", "O0", "O1", "am", "kO", "kC", "OHO", "wO", "so", "Q", "sP", "OHP", "ds", "OO",
-                   "ydf", "ycf", "yof"))
-SCRATCH.update(_sb("float32", "cv1", "cv2", "cv3", "cv4", w=384))
-SCRATCH.update(_sb("int32", "wti", "kq", w=1))
-SCRATCH.update(_sb("float32", "wtf", "K", "kc", w=1))
-SCRATCH.update(_sb("int32", "iP", "iC", "irow", "igp", "ich", "it0", "it1", "it2", "it3", "it4", w=24))
-SCRATCH.update(_sb("uint16", "dupi", "dupo", w=24))
-SCRATCH.update(_sb("uint16", "pick", "picko", "rep", "rep15", "aoff", w=12))
-SCRATCH.update(_sb("int32", "ei", "eu", "hiO", "eff", "lo", w=16))
-SCRATCH.update(_sb("float32", "vp", "thr", w=16))
-SCRATCH.update(_sb("uint16", "offs", w=16))
+XC = 3088 - 192 * min(RN, RC)
+MW = XC + 3088
+SCRATCH = {"zrow": ("sbuf", [2, 192], "bfloat16"), "crow": ("sbuf", [1, 192], "bfloat16"),
+           "orow": ("sbuf", [1, 192], "bfloat16")}
+SCRATCH.update(_sb("bfloat16", "xtw", w=WT))
+SCRATCH.update(_sb("bfloat16", "xph", w=2 * WT))
+SCRATCH.update(_sb("bfloat16", "cs", "cg", w=WT // 4))
+SCRATCH.update(_sb("bfloat16", "xo", "xa", "sa", "mo", "dx", w=3072))
+SCRATCH.update(_sb("bfloat16", "Iw", "mc", w=MW))
+SCRATCH.update(_sb("bfloat16", "d2", w=384))
+SCRATCH.update(_sb("float32", "baseN", "baseR", w=1))
+SCRATCH.update(_sb("bfloat16", "rsa", w=16 * VA))
+SCRATCH.update(_sb("bfloat16", "E", "NE", w=144))
+SCRATCH.update(_sb("bfloat16", "idn", "nid", "id4", "id16", "idg", "neg", "BO", "W2", "W8", w=128))
+SCRATCH.update(_sb("float32", "idf", "nidf", "BOf", w=128))
+SCRATCH.update(_sb("bfloat16", "ones", "rst", "gn", "ind", "tv", "up", "hq", "OHO", "DA", "DB"))
+SCRATCH.update(_sb("int32", "pki", "poi", "dmi", "pi", "pf", "ci", "cf", "mi", "mf", "sO", "sP"))
+SCRATCH.update(_sb("uint16", "offo", "offc", "offm"))
+SCRATCH.update(_sb("float32", "O0", "am", "vp", "wO", "Q", "tC", "OO", "hrep", "ydf", "yof"))
+SCRATCH.update(_sb("int32", "wti", w=1))
+SCRATCH.update(_sb("float32", "wtf", "cnt", "rb", "qf", "K", w=1))
+SCRATCH.update(_sb("bfloat16", "nkt", w=1))
+SCRATCH.update(_sb("int32", "iC", "iD", "iE", "iF", "iG", "iH", "jo", "lo", w=16))
+SCRATCH.update(_sb("uint16", "rep", "ju", "loc", "toB", "toA", w=16))
+SCRATCH.update(_sb("float32", "hi", "junk", w=16))
 SCRATCH.update(_sb("bfloat16", "sw", w=16))
-SCRATCH.update(_sb("float32", "nn", w=72))
-SCRATCH.update(_sb("float32", "ev", "evs", "ym", w=36))
-SCRATCH.update(_sb("int32", "yq", "yf", w=36))
-SCRATCH.update(_sb("uint16", "yoff", w=36))
 SCRATCH.update(_sb("float32", "cin", "cout", w=192 * NV))
-SCRATCH.update(_sb("float32", "rec", w=24 * (NV - 1)))
-SCRATCH.update(_sb("float32", "rin", w=72 * NV))
-PSUM = ("pd0", "pd1", "pkO", "pkA", "pkB", "pM1", "pM2", "pZ")
-SCRATCH.update({nm: ("psum", [128, 512], "float32") for nm in PSUM})
-SEMAPHORES = (["sv", "ss", "sp", "sg", "ls", "l_po", "l_dm", "l_pk", "l_wt", "l_xt", "s_yc", "s_yo", "s_yd"]
-              + ["arr%d" % t for t in range(1, NV)] + [nm + str(t) for t in range(4, NV) for nm in ("ra", "rb")])
+PSUM = ("pd0", "pd1", "Dp", "kO", "kC", "Z", "Op", "Cp")
+SCRATCH.update({nm: ("psum", [128, 512], "float32") for nm in PSUM[2:]})
+SCRATCH.update({nm: ("psum", [128, 32, 16], "float32") for nm in PSUM[:2]})
+SEMAPHORES = (["sv", "ss", "sp", "sg", "ls", "l_po", "l_dm", "l_pk", "l_wt", "l_xt", "l_w2", "l_p1", "l_p2", "l_ph",
+               "l_i0", "l_i1", "s_yc", "s_yo", "s_yd"] + ["arr%d" % t for t in range(1, NV)])
 
 
 def rank_program(g, core, T, topo):
@@ -71,7 +74,7 @@ def rank_program(g, core, T, topo):
             if known[q].get(k2, 0) < v2:
                 known[q][k2] = v2
 
-    def order(q, reads, writes):
+    def order(q, reads, writes, cont=False):
         deps = {}
 
         def add(tok, skip_own=False):
@@ -85,7 +88,7 @@ def rank_program(g, core, T, topo):
             if b in PSUM:
                 add(readers.get(b, {}), True)
         for b in writes:
-            add(last_w.get(b, {}), q == "p")
+            add(last_w.get(b, {}), q == "p" and not cont)
             add(readers.get(b, {}), True)
         for sm in sorted(deps):
             need(q, sm, deps[sm])
@@ -97,8 +100,8 @@ def rank_program(g, core, T, topo):
         for b in reads:
             readers.setdefault(b, {})[tok_sem] = tok_val
 
-    def op(q, fn, reads, writes):
-        order(q, reads, writes)
+    def op(q, fn, reads, writes, cont=False):
+        order(q, reads, writes, cont)
         sem = own[q]
         fn().then_inc(T.sem[sem], 1)
         count[sem] += 1
@@ -116,21 +119,16 @@ def rank_program(g, core, T, topo):
         readers[buf] = {}
 
     v, s, pe = g.vector, g.scalar, g.tensor
-    width = {"cin": 192, "cout": 192, "rec": 24, "rin": 72}
 
     def X(name):
-        base = name.rstrip("0123456789")
-        if base not in width:
-            return T[name][:]
-        w = width[base]
-        i = int(name[len(base):])
-        return T[base][:, w * i:w * i + w]
+        i = int(name[-1])
+        return T[name[:-1]][:, 192 * i:192 * i + 192]
 
     def V(fn, r, w):
         op("v", fn, r, w)
 
-    def copy_s(out, in_, r, w, f=F_.Copy):
-        op("s", lambda: s.activation(out, in_, f), r, w)
+    def act(out, in_, r, w, f=F_.Copy, **kw):
+        op("s", lambda: s.activation(out, in_, f, **kw), r, w)
 
     def copy_v(out, in_, r, w):
         V(lambda: v.tensor_copy(out, in_), r, w)
@@ -147,165 +145,182 @@ def rank_program(g, core, T, topo):
     def ts2(out, a, s1, s2, o0, o1, r, w):
         V(lambda: v.tensor_scalar(out, a, s1, s2, o0, o1), r, w)
 
-    def scan(out, d0, d1, o1, r, w):
-        V(lambda: v.tensor_tensor_scan(out, d0, d1, 0.0, A_.mult, o1), r, w)
+    def scan(out, d0, d1, o0, r, w):
+        V(lambda: v.tensor_tensor_scan(out, d0, d1, 0.0, o0, A_.max), r, w)
 
-    def mm(out, lhsT, rhs, st, sp, r, w):
-        op("p", lambda: pe.matmul(out, lhsT, rhs, st, sp), r, w)
+    def mm(out, lhsT, rhs, st, sp, r, w, cont=False):
+        op("p", lambda: pe.matmul(out, lhsT, rhs, st, sp), r, w, cont)
 
-    def blk(nm, c0, c1):
-        return ["%s%d" % (nm, c) for c in range(c0, c1)]
+    def select(out, in_, pat, cmp, fill_, base, cm, r, w):
+        op("g", lambda: g.affine_select(out, in_, pat, cmp, fill_, base, cm), r, w)
+
+    def iota(out, pat, base, cm, w, small=False):
+        if small:
+            op("g", lambda: g.iota(out, pat, base, cm, allow_small_or_imprecise_dtypes=True), [], w)
+        else:
+            op("g", lambda: g.iota(out, pat, base, cm), [], w)
+
+    def part(nm, a, b):
+        return ["%s%d" % (nm, u) for u in range(a // 4, (b + 3) // 4)]
 
     dma("y", T.dmi[:], T.dm[:], "l_dm", [], ["dmi"])
-    dma("y", T.poi[:], T.po[:], "l_po", [], ["poi"])
+    dma("s", T.xtw[:, 0:4096], T.xt[:], "l_xt", [], ["xtw"])
     dma("y", T.wti[:], T.wt[:], "l_wt", [], ["wti"])
-    dma("s", T.xtw[:, TAB:TAB + 4096], T.xt[:], "l_xt", [], ["xtw"])
+    dma("y", T.poi[:], T.po[:], "l_po", [], ["poi"])
+    dma("y", T.xtw[:, 4096:WT], T.xt[:, 0:32], "l_w2", [], ["xt_wrap"])
     dma("y", T.pki[:], T.pk[:], "l_pk", [], ["pki"])
-    fill(T.bd8[:], 4096.0, ["bd8"])
+    XT = ["xtw", "xt_wrap"]
+    dma("y", T.xph[:, 0:WT], T.xtw[:], "l_p1", XT, ["xph_a"])
+    dma("y", T.xph[:, WT:2 * WT], T.xtw[:], "l_p2", XT, ["xph_b"])
     fill(T.ones[:], 1.0, ["ones"])
+    iota(T.iD[:], [[-1, 16]], 128, 1, ["iD"])
+    iota(T.iC[:], [[1, 16]], 0, 0, ["iC"])
     fill(T.E[:], 0.0, ["E"])
-    op("g", lambda: g.affine_select(T.bd8[:], T.bd8[:], [[-16, 8]], A_.is_ge, 0.0, 0, 1), ["bd8"], ["bd8"])
-    op("g", lambda: g.affine_select(T.bd8[:], T.bd8[:], [[16, 8]], A_.is_ge, 0.0, 15, -1), ["bd8"], ["bd8"])
-    op("g", lambda: g.iota(T.iP[:], [[0, 24]], 0, 1), [], ["iP"])
-    op("g", lambda: g.iota(T.iC[:], [[1, 24]], 0, 0), [], ["iC"])
-    op("g", lambda: g.affine_select(T.idn[:], T.ones[:, 0:128], [[-1, 128]], A_.is_equal, 0.0, 0, 1), ["ones"], ["idn"])
-    op("g", lambda: g.iota(T.rrow[:], [[0, 8], [1, 16]], 0, 0, allow_small_or_imprecise_dtypes=True), [], ["rrow"])
-    op("g", lambda: g.iota(T.c16[:], [[16, 192]], 0, 0, allow_small_or_imprecise_dtypes=True), [], ["c16"])
-    for r in range(16):
-        copy_s(T.E[:, r * 129:(r + 1) * 128:16], T.bd8[:], ["bd8", "E"], ["E%d" % r])
-    EA = ["E"] + blk("E", 0, 16)
-    ts(T.irow[:], T.iP[:], 15, A_.bitwise_and, ["iP"], ["irow"])
-    ts(T.ich[:], T.iC[:], 1, A_.logical_shift_right, ["iC"], ["ich"])
-    ts2(T.igp[:], T.iP[:], 4, 1, A_.logical_shift_right, A_.bitwise_and, ["iP"], ["igp"])
-    ts(T.it0[:], T.ich[:], 16, A_.mult, ["ich"], ["it0"])
-    copy_v(T.D0[:], T.dmi[:], ["dmi"], ["D0"])
-    tt(T.it1[:], T.it0[:], T.irow[:], A_.add, ["it0", "irow"], ["it1"])
-    ts(T.igp[:], T.igp[:], 16, A_.mult, ["igp"], ["igp"])
-    copy_v(T.dupi[:], T.it1[:], ["it1"], ["dupi"])
-    ts2(T.it2[:, 0:12], T.iC[:, 0:12], 32, 15, A_.mult, A_.add, ["iC"], ["it2"])
-    tt(T.it3[:, 0:12], T.igp[:, 0:12], T.irow[:, 0:12], A_.subtract, ["igp", "irow"], ["it3"])
-    copy_v(T.rep[:], T.iC[:, 0:12], ["iC"], ["rep"])
-    tt(T.it2[:, 0:12], T.it2[:, 0:12], T.it3[:, 0:12], A_.add, ["it2", "it3"], ["it2"])
-    ts(T.wtf[:], T.wti[:], 1.0 / 2048, A_.mult, ["wti"], ["wtf"])
-    copy_v(T.pick[:], T.it2[:, 0:12], ["it2"], ["pick"])
-
-    def seat_in(src, dst, a, b):
-        copy_v(T[a][:], T[src][:].indirect(T.dupi[:]), [src, "dupi"], [a])
-        V(lambda: v.transpose(T[b][:], T[a][:]), [a], [b])
-        copy_v(X(dst), T[b][:].indirect(T.pick[:]), [b, "pick"], [dst])
-
-    def seat_out(src, dst, a, b, out, sem, q, cp):
-        cp(T[a][:], X(src).indirect(T.dupo[:]), [src, "dupo"], [a])
-        V(lambda: v.transpose(T[b][:], T[a][:]), [a], [b])
-        cp(T[dst][:], T[b][:].indirect(T.picko[:]), [b, "picko"], [dst])
-        dma(q, out[:], T[dst][:], sem, [dst], [])
-
-    seat_in("poi", "O0", "cv1", "cv2")
-    ts(T.WE[:], T.E[:], T.wtf[:, 0:1], A_.mult, EA + ["wtf"], ["WE"])
+    fill(T.zrow[0:2, :], float(ZB), ["zrow"])
+    fill(T.E[:, 15:143:16], 4096.0, ["E"])
+    fill(T.zrow[0:1, :], 33.0, ["zrow"])
+    select(T.BO[:], T.ones[:, 0:128], [[-16, 8], [0, 16]], A_.is_ge, 0.0, 0, 1, ["ones"], ["BO"])
+    select(T.idn[:], T.ones[:, 0:128], [[-1, 128]], A_.is_equal, 0.0, 0, 1, ["ones"], ["idn"])
+    select(T.BO[:], T.BO[:], [[16, 8], [0, 16]], A_.is_ge, 0.0, 15, -1, ["BO"], ["BO"])
+    select(T.E[:, 15:143:16], T.E[:, 15:143:16], [[-16, 8]], A_.is_ge, 0.0, 0, 1, ["E"], ["E"])
+    iota(T.orow[:], [[0, 12], [-1, 16]], 15, 0, ["orow"], True)
+    select(T.E[:, 15:143:16], T.E[:, 15:143:16], [[16, 8]], A_.is_ge, 0.0, 15, -1, ["E"], ["E"])
+    iota(T.crow[:], [[-1, 192]], 0, 0, ["crow"], True)
     fill(T.K[:], 0.0, ["K"])
-    ts(T.nid[:], T.idn[:], -1.0, A_.mult, ["idn"], ["nid"])
-    fill(T.c3k[:], 3072.0, ["c3k"])
-    fill(T.cff[:], 4096.0 * 4080, ["cff"])
-    fill(T.cff[:, 68:72], 0.0, ["cff"])
+    ts(T.iE[:], T.iD[:], 15, A_.bitwise_and, ["iD"], ["iE"])
+    copy_v(T.qf[:], T.iE[:, 0:1], ["iE"], ["qf"])
+    ts2(T.iF[:], T.iC[:], 16.0, T.qf[:, 0:1], A_.mult, A_.add, ["iC", "qf"], ["iF"])
+    ts2(T.iG[:], T.iF[:], -5.5, 1.0 / 12, A_.add, A_.mult, ["iF"], ["iG"])
+    ts(T.iH[:], T.iF[:], 16.0, A_.mult, ["iF"], ["iH"])
+    ts(T.iG[:], T.iG[:], -191.0, A_.mult, ["iG"], ["iG"])
+    ts(T.wtf[:], T.wti[:], 2.0, A_.mult, ["wti"], ["wtf"])
+    tt(T.iH[:], T.iH[:], T.iG[:], A_.add, ["iH", "iG"], ["iH"])
+    copy_v(T.DA[:], T.dmi[:], ["dmi"], ["DA"])
+    copy_v(T.toB[:], T.iH[:], ["iH"], ["toB"])
+    ts(T.W2[:], T.BO[:], T.wtf[:, 0:1], A_.mult, ["BO", "wtf"], ["W2"])
+    act(T.idf[:], T.idn[:], ["idn"], ["idf"])
+    copy_v(T.O0[:], T.poi[:], ["poi"], ["O0"])
 
     def constants_1():
-        ts(T.NE[:], T.E[:], -1.0, A_.mult, EA, ["NE"])
-        fill(T.mc[:, 3072:3088], 512.0, ["mc_end"])
-        fill(T.Dt[:, 128:192], 0.0, ["Dt0"])
-        ts(T.id4[:], T.idn[:], -4.0, A_.mult, ["idn"], ["id4"])
+        ts(T.nid[:], T.idn[:], -1.0, A_.mult, ["idn"], ["nid"])
+        ts(T.NE[:], T.E[:], -1.0, A_.mult, ["E"], ["NE"])
+        for nm, rv in (("baseN", RN), ("baseR", RC)):
+            ts2(T[nm][:], T.qf[:], rv - 0.5, float(XC), A_.is_gt, A_.mult, ["qf"], [nm])
+            ts(T[nm][:], T[nm][:], 3072.0, A_.add, [nm], [nm])
+        copy_v(X("cin0"), T.pki[:], ["pki"], ["cin0"])
+        fill(T.rsa[:], 0.0, ["rsa"])
+        copy_v(T.rep[:], T.iC[:], ["iC"], ["rep"])
+        fill(T.rsa[:, 0:16 * VA:16], -2.0 ** 26, ["rsa"])
+        ts(T.Iw[:, 0:16], T.iE[:], 0.0, A_.is_equal, ["iE"], ["Iw0"])
+        ts2(T.rb[:], T.qf[:], -192.0, -1024.0, A_.mult, A_.add, ["qf"], ["rb"])
+        for a in (3072, XC + 3072):
+            fill(T.Iw[:, a:a + 16], 0.0, ["Iw_end%d" % a])
+            fill(T.mc[:, a:a + 16], -1.0, ["mc_end%d" % a])
         fill(T.rst[:], 1.0, ["rst"])
+        ts(T.id4[:], T.idn[:], -4.0, A_.mult, ["idn"], ["id4"])
         fill(T.rst[:, 0:192:16], 0.0, ["rst"])
-        ts2(T.it4[:, 0:12], T.iC[:, 0:12], 16, 15, A_.mult, A_.add, ["iC"], ["it4"])
-        copy_v(T.rep15[:], T.it4[:, 0:12], ["it4"], ["rep15"])
+        ts(T.W8[:], T.W2[:], -4.0, A_.mult, ["W2"], ["W8"])
+        w = 16
+        while w < 1536:
+            d = min(w, 1536 - w)
+            select(T.Iw[:, w:w + d], T.Iw[:, 0:d], [[0, d]], A_.is_ge, 0.0, 0, 0, ["Iw0", "Iw"], ["Iw"])
+            w += d
+        for i, (a, b) in enumerate(((1536, 3072), (3088, MW - 16))):
+            dma("y", T.Iw[:, a:b], T.Iw[:, 0:b - a], "l_i%d" % i, ["Iw0", "Iw"], ["Iw_c%d" % i])
+        if RN > RC:
+            fill(T.mc[:, XC + 192 * RC:XC + 192 * RN], 0.0, part("xc", 12 * RC, 12 * RN))
+        act(T.nidf[:], T.idn[:], ["idn"], ["nidf"], scale=-1.0)
+        act(T.BOf[:], T.BO[:], ["BO"], ["BOf"])
 
     def constants_2():
-        fill(T.xtw[:, 0:TAB], -1.0, ["xt_m1"])
         fill(T.neg[:], -0.0625, ["neg"])
         ts(T.id16[:], T.idn[:], 16.0, A_.mult, ["idn"], ["id16"])
-        ts2(T.it2[:, 0:12], T.iC[:, 0:12], 256, 240, A_.mult, A_.add, ["iC"], ["it2"])
-        tt(T.it2[:, 0:12], T.it2[:, 0:12], T.irow[:, 0:12], A_.add, ["it2", "irow"], ["it2"])
-        copy_v(T.aoff[:], T.it2[:, 0:12], ["it2"], ["aoff"])
+        ts(T.idg[:], T.idn[:], float(WT), A_.mult, ["idn"], ["idg"])
+        ts(T.wtf[:], T.qf[:], 12.0, A_.mult, ["qf"], ["wtf"])
+        ts(T.toA[:], T.iC[:], T.wtf[:, 0:1], A_.add, ["iC", "wtf"], ["toA"])
 
-    def constants_3():
-        ts(T.it1[:], T.it0[:], 15, A_.add, ["it0"], ["it1"])
-        tt(T.it1[:], T.it1[:], T.irow[:], A_.subtract, ["it1", "irow"], ["it1"])
-        copy_v(T.dupo[:], T.it1[:], ["it1"], ["dupo"])
-        ts(T.it4[:, 0:12], T.iC[:, 0:12], 32, A_.mult, ["iC"], ["it4"])
-        tt(T.it4[:, 0:12], T.it4[:, 0:12], T.irow[:, 0:12], A_.add, ["it4", "irow"], ["it4"])
-        tt(T.it4[:, 0:12], T.it4[:, 0:12], T.igp[:, 0:12], A_.add, ["it4", "igp"], ["it4"])
-        copy_v(T.picko[:], T.it4[:, 0:12], ["it4"], ["picko"])
+    def return_tables(half):
+        nm, c, piece = (("cs", -127.5, "xph_a"), ("cg", -128.0, "xph_b"))[half]
+        q = WT // 4
+        select(T[nm][:], T.xtw[:, 0:q], [[0, q]], A_.is_gt, c, 0, 0, XT, [nm])
+        order("g", [nm], [piece])
+        for i in range(4):
+            a = half * WT + i * q
+            g.dma_start(T.xph[:, a:a + q], T[nm][:], accum_op=A_.add).then_inc(T.sem.l_ph, 16)
+        if half:
+            arrived("xph", "l_ph", 128)
 
-    win = T.xtw[:, TAB:WEND]
-    winm = T.xtw[:, 0:WEND]
-    XT = ["xtw", "xt_wrap"]
-    XTM = ["xtw", "xt_wrap", "xt_m1"]
-    DX = blk("dx", 0, 16)
+    win = T.xtw[:]
+    Dp = T.Dp[:, 0:192]
+    nu = T.Cp[:, 192:384]
+    DX = ["dx%d" % k for k in range(16)]
 
-    def E(r):
-        return T.E[:, r * 128:(r + 1) * 128]
+    def E(nm, r):
+        return T[nm][:, 15 - r:143 - r]
 
-    def emit_e(dn):
-        for r in range(16):
-            mm(T.pM2[:, 0:12], T.WE[:, r * 128:(r + 1) * 128], T[dn][:, r:192:16], r == 0, r == 15, ["WE", dn], ["pM2"])
+    def start_z(stop):
+        mm(T.Z[:, 0:192], T.ones[0:2, 0:128], T.zrow[:], True, False, ["ones", "zrow"], ["Z"])
+        mm(T.Z[:, 0:192], T.W2[:], T.DA[:], False, stop, ["W2", "DA"], ["Z"])
 
     def emit_v():
-        copy_v(T.ei[:, 0:12], T.pM2[:, 0:12], ["pM2"], ["ei"])
-        ts(T.eu[:, 0:12], T.ei[:, 0:12], 2047, A_.bitwise_and, ["ei"], ["eu"])
-        ts(T.vp[:, 0:12], T.eu[:, 0:12], 33.0, A_.add, ["eu"], ["vp"])
+        ts(T.hq[:], T.Z[:, 0:192], -1056.0, A_.add, ["Z"], ["hq"])
+        tt(T.vp[:], T.Z[:, 0:192], T.hq[:], A_.subtract, ["Z", "hq"], ["vp"])
 
-    def columns(cards, a, b):
-        tt(T[a][:], T.vp[:, 0:12].indirect(T.rep[:]), X(cards), A_.mult, ["vp", "rep", cards], [a])
+    def columns(cards, bank, a, b):
+        tt(T[a][:], cards, T.vp[:], A_.mult, ["vp", bank], [a])
         ts2(T[b][:], T[a][:], 5, 4095, A_.arith_shift_right, A_.bitwise_and, [a], [b])
 
-    def emit_list(cards, a, b, off):
-        columns(cards, a, b)
-        ts(T[off][:], T[b][:], T.K[:, 0:1], A_.add, [b, "K"], [off])
+    def add_k(off, b):
+        ts(T[off][:], T[b][:].indirect(T.toB[:, 0:12]), T.K[:, 0:1], A_.add, [b, "toB", "K"], [off])
 
-    def emit_dx(dn, onv):
-        for k in range(16):
-            (copy_v if k in onv else copy_s)(T.dx[:, :, 16 * k:16 * k + 16], T[dn][:], [dn], ["dx%d" % k])
+    def copy_g(out, in_, r, w):
+        select(out, in_, [[0, in_.shape[1]]], A_.is_ge, 0.0, 0, 0, r, w)
 
-    def emit_sd(dn):
-        mm(T.pkO[:, 192:204], T.ones[0:1, 0:128], T.c3k[0:1, 0:12], True, False, ["ones", "c3k"], ["pkO"])
-        mm(T.pkO[:, 192:204], T.ones[0:1, 0:128], T.cff[0:1, 64:76], False, False, ["ones", "cff"], ["pkO"])
-        for r in range(16):
-            mm(T.pkO[:, 196:200], E(r), T[dn][:, 64 + r:128:16], False, r == 15, ["E%d" % r, dn], ["pkO"])
+    def spread(cp, ks, rv):
+        for k in ks:
+            cp(T.dx[:, k:192 * rv:16], T.DB[:, 0:12 * rv], ["DB"], ["dx%d" % k])
 
-    def gather(onv, dst, off, c0, c1, w=None):
-        o = T[dst][:, 256 * c0:256 * c1]
-        i = (w or win).indirect(T[off][:, 16 * c0:16 * c1])
-        (copy_v if onv else copy_s)(o, i, (XTM if w is not None else XT) + [off], blk(dst, c0, c1))
+    def twice(cp, rv):
+        for k in range(2):
+            cp(T.d2[:, 24 * rv + k:384:2], T.DB[:, 12 * rv:192], ["DB"], ["d2%d" % k])
 
-    def fused(dst, off, c0, c1):
-        for c in range(c0, c1):
-            tt(T[dst][:, 256 * c:256 * c + 256], win.indirect(T[off][:, 16 * c:16 * c + 16]), T.dx[:, c, :], A_.min,
-               XT + [off] + DX, ["%s%d" % (dst, c)])
+    def lanes(nm, a, b):
+        return T.mc[:, XC + 16 * a:XC + 16 * b] if nm == "xc" else T[nm][:, 16 * a:16 * b]
 
-    def minus_x(j, src):
-        b = "pd%d" % (j % 2)
-        mm(T[b][:], T.nid[:], T[src][:, 512 * j:512 * j + 512], True, False, ["nid"] + blk(src, 2 * j, 2 * j + 2), [b])
+    def gather(onv, dst, off, a, b, w=None):
+        i = (w or win).indirect(T[off][:, a:b])
+        (copy_v if onv else act)(lanes(dst, a, b), i, (["xph"] if w is not None else XT) + [off], part(dst, a, b))
 
-    def plus_d(j, dst):
-        b = "pd%d" % (j % 2)
-        mm(T[b][:, 0:256], T.idn[:], T.dx[:, 2 * j, :], False, False, ["idn"] + DX, [b])
-        mm(T[b][:, 256:512], T.idn[:], T.dx[:, 2 * j + 1, :], False, True, ["idn"] + DX, [b])
-        copy_s(T[dst][:, 512 * j:512 * j + 512], T[b][:], [b], blk(dst, 2 * j, 2 * j + 2), F_.Relu)
+    def fused(dst, off, r0, r1):
+        a, b = 12 * r0, 12 * r1
+        tt(lanes(dst, a, b), win.indirect(T[off][:, a:b]), lanes("dx", a, b), A_.min, XT + [off] + DX, part(dst, a, b))
 
-    def pair(j, src, dst):
-        minus_x(j, src)
-        plus_d(j, dst)
+    turn = [0]
 
-    def bias(bank, lo, hi, ff):
-        mm(T[bank][:, 0:hi - lo], T.ones[0:1, 0:128], T.c16[0:1, lo:hi], True, False, ["ones", "c16"], [bank])
-        mm(T[bank][:, 0:hi - lo], T.rrow[0:1, :], T.ones[0:1, 0:hi - lo], False, False, ["ones", "rrow"], [bank])
-        if ff:
-            mm(T[bank][:, 0:ff], T.ones[0:1, 0:128], T.cff[0:1, 0:ff], False, False, ["ones", "cff"], [bank])
+    where = {}
 
-    def score(bank, src, c0, at, neg, final):
-        for r in range(16):
-            mm(T[bank][:, at:at + 64], T.NE[:, r * 128:(r + 1) * 128] if neg else E(r),
-               T[src][:, 256 * c0 + r:256 * c0 + 1024:16], False, final and r == 15,
-               ["NE" if neg else "E%d" % r] + blk(src, c0, c0 + 4), [bank])
+    def minus_x(src, a, b):
+        bank = where[a] = "pd%d" % (turn[0] % 2)
+        turn[0] += 1
+        mm(T[bank][:, 0:b - a, :], T.nid[:], lanes(src, a, b), True, False, ["nid"] + part(src, a, b), [bank])
+
+    def plus_d(a, b):
+        bank = where[a]
+        for k in range(0, 16, 2):
+            mm(T[bank][:, 0:b - a, k:k + 2], T.idn[:], T.d2[:, 2 * a:2 * b], False, k == 14, ["idn", "d20", "d21"], [bank])
+
+    def minus(src, a, b):
+        minus_x(src, a, b)
+        plus_d(a, b)
+
+    def relu(dst, a, b):
+        act(lanes(dst, a, b), T[where[a]][:, 0:b - a, :], [where[a]], part(dst, a, b), F_.Relu)
+
+    def score(bank, src, r0, r1, neg, final=False):
+        nm = "NE" if neg else "E"
+        for r in range(r0, r1):
+            mm(T[bank][:, 0:192], E(nm, r), T[src][:, 192 * r:192 * r + 192], False, final and r == r1 - 1,
+               [nm] + part(src, 12 * r, 12 * r + 12), [bank])
 
     def send_pack(t):
         dst = T.cores[(rank + 1) % n]
@@ -316,209 +331,267 @@ def rank_program(g, core, T, topo):
                      sum(1 << e for e in eng))
         return len(eng)
 
-    def send_rec(q):
-        need("g", *list(last_w["rec%d" % q].items())[0])
-        trs = []
-        for d in (1, 2, 3):
-            t = q + d
-            if t < 4 or t >= NV:
-                continue
-            dst = T.cores[(rank + d) % n]
-            rid, pid = topo.addr(dst, core)
-            eng = topo.engines(core, dst)[2 * len(trs):2 * len(trs) + 2]
-            b = 72 * t + 24 * (q - (t - 3))
-            trs.append(RemoteDMATransfer(dst_ids=[DstId(rid=rid, pnc=pid)], dma_engine_mask=sum(1 << e for e in eng),
-                                         remote_sem=T.sem[("rb%d" if d == 1 else "ra%d") % t], srcs=[X("rec%d" % q)],
-                                         dsts=[T.rin[:, b:b + 24]]))
-        if trs:
-            g.remote_dma_fused(trs, local_sem=T.sem.ls)
-        return 2 * len(trs)
+    def start_d():
+        act(nu, T.DA[:], ["DA"], ["Cp"], F_.Relu, scale=-1.0, bias=5.0)
+        mm(Dp, T.idn[:], T.DA[:], True, False, ["idn", "DA"], ["Dp"])
+        start_z(False)
+
+    def pack_in(t):
+        if t > 0:
+            arrived("cin%d" % t, "arr%d" % t, 8)
+        mm(T.Cp[:, 0:192], T.idf[:], X("cin%d" % t), True, True, ["idf", "cin%d" % t], ["Cp"])
+
+    def pool_choice():
+        scan(T.sO[:], T.rsa[:, 0:192], T.kO[:, 0:192], A_.add, ["rsa", "kO"], ["sO"])
+        ts(T.jo[:, 0:12], T.sO[:, 15:192:16], 15, A_.bitwise_and, ["sO"], ["jo"])
+        ts2(T.hi[:, 0:12], T.sO[:, 15:192:16], 1.5 * 2.0 ** 35, 1.5 * 2.0 ** 35, A_.add, A_.subtract, ["sO"], ["hi"])
+        ts2(T.ju[:, 0:12], T.jo[:, 0:12], -1.0, 15.0, A_.mult, A_.add, ["jo"], ["ju"])
+
+    def pool_hot():
+        act(T.OHO[:], T.Iw[:, 0:16].indirect(T.ju[:, 0:12]), ["Iw0", "ju"], ["OHO"])
+        act(T.hrep[:], T.hi[:, 0:12].indirect(T.rep[:, 0:12]), ["hi", "rep", "rb"], ["hrep"], F_.Identity, bias=T.rb[:, 0:1])
+
+    def pool_card(t):
+        tt(T.wO[:], T.OHO[:], T.Op[:, 0:192], A_.mult, ["OHO", "Op"], ["wO"])
+        mm(T.kO[:, 192:384], T.nidf[:], X("cin%d" % t), True, False, ["nidf", "cin%d" % t], ["kO"])
+        mm(T.kO[:, 192:384], T.BOf[:], T.wO[:], False, True, ["BOf", "wO"], ["kO"])
+
+    def bias_o():
+        mm(T.kO[:, 0:192], T.ones[0:1, 0:128], T.orow[:], True, False, ["ones", "orow"], ["kO"])
+
+    def bias_c():
+        mm(T.kC[:, 0:192], T.ones[0:1, 0:128], T.crow[:], True, False, ["ones", "crow"], ["kC"])
+
+    def thr_c():
+        mm(T.kC[:, 0:192], T.idf[:], T.hrep[:], False, False, ["idf", "hrep"], ["kC"])
+
+    def thirds(a, b):
+        w = (b - a + 11) // 12 * 4
+        return [(a, a + w), (a + w, a + 2 * w), (a + 2 * w, b)]
+
+    def runs(a, b):
+        k = (b - a + 31) // 32
+        w = ((b - a + k - 1) // k + 3) // 4 * 4
+        return [(x, min(x + w, b)) for x in range(a, b, w)]
+
+    def demands_to_dx(full):
+        act(T.DB[:], T.DA[:].indirect(T.toB[:, 0:12]), ["DA", "toB"], ["DB"])
+        if full:
+            spread(act, range(0, KS), RN)
+            spread(copy_g, range(KS, KS + KG), RN)
+            twice(act, RN)
 
     left = 0
-    dcur, ocur = "D0", "O0"
-    emit_e("D0")
+    start_z(True)
+    mm(T.Op[:, 0:192], T.idf[:], T.O0[:], True, True, ["idf", "O0"], ["Op"])
+    demands_to_dx(True)
     emit_v()
-    emit_dx("D0", ())
-    copy_s(T.xtw[:, TAB + 4096:WEND], T.xtw[:, TAB:TAB + 32], ["xtw"], ["xt_wrap"])
+    columns(T.Op[:, 0:192], "Op", "pi", "pf")
+    add_k("offo", "pf")
+    spread(copy_v, range(KS + KG, 16), RN)
     for t in range(NV):
         back = t >= 4
         last = t == NV - 1
         c_in, c_out, mback = "cin%d" % t, "cout%d" % t, "cout%d" % (t - 4)
-        onx = "O1" if t % 2 == 0 else "O0"
-        emit_list(ocur, "pi", "pf", "offo")
-        gather(False, "xo", "offo", 4, 6)
-        copy_s(T.pZ[:, 0:192], X(ocur), [ocur], ["pZ"])
-        if back:
-            copy_s(T.pZ[:, 192:384], X(mback), [mback], ["pZ"])
-        gather(False, "xo", "offo", 6, 8)
         if not back:
-            emit_sd(dcur)
-            pair(2, "xo", "mo")
+            rv = RN
+            S = thirds(12 * rv, 192)
+            done = [rv] + [b // 12 for a, b in S]
+            o1, o2, c1, c2, c3 = CUTN
             if t == 0:
                 constants_1()
-                seat_in("pki", "cin0", "cv3", "cv4")
-            fused("mo", "offo", 0, 4)
-            gather(False, "xo", "offo", 8, 10)
-            pair(3, "xo", "mo")
-            gather(False, "xo", "offo", 10, 12)
+            gather(False, "xo", "offo", *S[0])
+            fused("mo", "offo", 0, o1)
+            gather(False, "xo", "offo", *S[1])
+            bias_o()
+            minus("xo", *S[0])
+            relu("mo", *S[0])
+            minus("xo", *S[1])
+            pack_in(t)
+            fused("mo", "offo", o1, o2)
+            score("kO", "mo", 0, o1, True)
+            score("kO", "mo", done[0], done[1], False)
+            gather(False, "xo", "offo", *S[2])
+            relu("mo", *S[1])
+            minus("xo", *S[2])
+            relu("mo", *S[2])
+            if t in (1, 2):
+                need("g", "arr%d" % t, 8)
+                return_tables(t - 1)
+            columns(T.Cp[:, 0:192], "Cp", "ci", "cf")
+            add_k("offc", "cf")
+            score("kO", "mo", o1, o2, True)
+            score("kO", "mo", done[1], done[3], False)
+            start_d()
+            fused("mo", "offo", o2, rv)
+            gather(False, "xc", "offc", *S[0])
+            minus("xc", *S[0])
+            score("kO", "mo", o2, rv, True, True)
+            fused("mc", "offc", 0, c1)
+            gather(False, "xc", "offc", *S[1])
+            relu("mc", *S[0])
+            minus("xc", *S[1])
             if t == 1:
                 constants_2()
-            if t == 2:
-                constants_3()
-            if t > 0:
-                arrived(c_in, "arr%d" % t, 8)
-            emit_list(c_in, "ci", "cf", "offc")
-            bias("pkO", 0, 192, 64)
-            score("pkO", "mo", 0, 0, True, False)
-            pair(4, "xo", "mo")
-            score("pkO", "mo", 4, 64, False, False)
-            pair(5, "xo", "mo")
-            gather(False, "xc", "offc", 8, 10)
-            fused("mc", "offc", 0, 4)
-            bias("pkA", 0, 128, 0)
-            score("pkA", "mc", 0, 0, False, False)
-            score("pkO", "mo", 8, 128, False, True)
-            gather(False, "xc", "offc", 10, 12)
-            copy_s(T.kO[:], T.pkO[:, 0:192], ["pkO"], ["kO"])
-            pair(4, "xc", "mc")
-            fused("mc", "offc", 4, 8)
-            pair(5, "xc", "mc")
+            pool_choice()
+            bias_c()
+            score("kC", "mc", done[0], done[1], True)
+            score("kC", "mc", 0, c1, False)
+            fused("mc", "offc", c1, c2)
+            gather(False, "xc", "offc", *S[2])
+            pool_hot()
+            minus("xc", *S[2])
+            pool_card(t)
+            thr_c()
+            relu("mc", *S[1])
+            relu("mc", *S[2])
+            fused("mc", "offc", c2, c3)
+            score("kC", "mc", c1, c2, False)
+            act(T.Q[:], T.kO[:, 192:384], ["kO"], ["Q"])
+            score("kC", "mc", done[1], done[3], True)
+            fused("mc", "offc", c3, rv)
+            score("kC", "mc", c2, c3, False)
+            score("kC", "mc", c3, rv, False, True)
         else:
-            gather(False, "xo", "offo", 8, 12)
-            P = [T.rin[:, 72 * t + 24 * i:72 * t + 24 * i + 12] for i in range(3)]
-            C = [T.rin[:, 72 * t + 24 * i + 12:72 * t + 24 * i + 24] for i in range(3)]
-            arrived("old", "ra%d" % t, 4)
-            arrived("new", "rb%d" % t, 2)
+            rv = RC
+            So, Sc = runs(12 * RP, 192), runs(12 * RC, 192)
+            gather(False, "xo", "offo", 12 * RP, XE)
+            columns(T.kC[:, 192:384], "kC", "mi", "mf")
+            gather(True, "xo", "offo", XF, 192)
+            mm(Dp, T.neg[:], T.ones[:], True, False, ["neg", "ones"], ["Dp"])
+            mm(Dp, T.idn[:], T.DB[:], False, False, ["idn", "DB"], ["Dp"])
             arrived(c_in, "arr%d" % t, 8)
-
-            def first(i, r):
-                tt(T.yq[:, 12 * i:12 * i + 12], T.vp[:, 0:12], C[i], A_.mult, ["vp", r], ["yq%d" % i])
-            columns(mback, "mi", "mf")
-            ts2(T.nn[:, 0:48], T.rin[:, 72 * t:72 * t + 48], 3072.0, BIG, A_.is_ge, A_.mult, ["old"], ["nna"])
-            tt(T.ev[:, 0:12], P[0], P[1], A_.is_equal, ["old"], ["ev0"])
-            first(0, "old")
-            first(1, "old")
-            tt(T.gn[:], X(c_in), T.pZ[:, 192:384], A_.not_equal, [c_in, "pZ"], ["gn"])
-            ts(T.pM2[:, 128:320], T.gn[:], BIG, A_.mult, ["gn"], ["pM2"])
-            tt(T.am[:], T.mf[:], T.pM2[:, 128:320], A_.add, ["mf", "pM2"], ["am"])
-            ts2(T.offa[:], T.am[:], T.K[:, 0:1], float(TAB), A_.add, A_.add, ["am", "K"], ["offa"])
-            va = 12 - VA
-            for c in range(0, va, 3):
-                gather(False, "xa", "offa", c, min(c + 3, va), winm)
-            emit_list(c_in, "ci", "cf", "offc")
-            ts2(T.nn[:, 48:72], T.rin[:, 72 * t + 48:72 * t + 72], 3072.0, BIG, A_.is_ge, A_.mult, ["new"], ["nnb"])
-            tt(T.ev[:, 12:24], P[0], P[2], A_.is_equal, ["old", "new"], ["ev1"])
-            tt(T.ev[:, 24:36], P[1], P[2], A_.is_equal, ["old", "new"], ["ev2"])
-            first(2, "new")
-            ts(T.evs[:], T.ev[:], BIG, A_.mult, blk("ev", 0, 3), ["evs"])
-            ts2(T.yf[:], T.yq[:], 5, 4095, A_.arith_shift_right, A_.bitwise_and, blk("yq", 0, 3), ["yf"])
-            for i in range(3):
-                tt(T.ym[:, 12 * i:12 * i + 12], T.yf[:, 12 * i:12 * i + 12], T.nn[:, 24 * i:24 * i + 12], A_.add,
-                   ["yf", "nna" if i < 2 else "nnb"], ["ym%d" % i])
-            tt(T.ym[:, 12:36], T.ym[:, 12:36], T.evs[:, 0:24], A_.add, ["ym1", "ym2", "evs"], ["ym1", "ym2"])
-            tt(T.ym[:, 24:36], T.ym[:, 24:36], T.evs[:, 24:36], A_.add, ["ym2", "evs"], ["ym2"])
-            ts2(T.yoff[:], T.ym[:], T.K[:, 0:1], float(TAB), A_.add, A_.add, blk("ym", 0, 3) + ["K"], ["yoff"])
-            if VA:
-                gather(True, "xa", "offa", va, 12, winm)
-            copy_v(T.yb0[:], winm.indirect(T.yoff[:, 0:12]), XTM + ["yoff"], ["yb0"])
-            tt(T.yb1[:], winm.indirect(T.yoff[:, 12:24]), T.yb0[:], A_.max, XTM + ["yoff", "yb0"], ["yb1"])
-            tt(T.yb2[:], winm.indirect(T.yoff[:, 24:36]), T.yb1[:], A_.max, XTM + ["yoff", "yb1"], ["yb2"])
-            gather(False, "xc", "offc", 8, 12)
-            mm(T.pM1[:, 0:192], T.neg[:], T.ones[:], True, False, ["neg", "ones"], ["pM1"])
-            mm(T.pM1[:, 0:192], T.idn[:], T[dcur][:], False, False, ["idn", dcur], ["pM1"])
-            minus_x(2, "xo")
-            minus_x(3, "xo")
-            for r in range(16):
-                scan(T.sa[:, r:3072:16], T.rst[:], T.xa[:, r:3072:16], A_.max, ["rst"] + blk("xa", 0, 12), ["sa%d" % r])
-            tt(T.up[:], T.sa[:].indirect(T.aoff[:]), T.yb2[:], A_.is_ge, blk("sa", 0, 16) + ["aoff", "yb2"], ["up"])
-            mm(T.pM1[:, 0:192], T.id16[:], T.up[:], False, True, ["id16", "up"], ["pM1"])
-            ts2(T.D2[:], T.pM1[:, 0:192], 1.0, 255.0, A_.max, A_.min, ["pM1"], ["D2"])
-            dcur = "D2"
-            emit_sd(dcur)
-            emit_dx(dcur, range(VDX))
-            fused("mo", "offo", 0, 4)
-            plus_d(2, "mo")
-            plus_d(3, "mo")
-            pair(4, "xo", "mo")
-            bias("pkO", 0, 192, 64)
-            score("pkO", "mo", 0, 0, True, False)
-            pair(5, "xo", "mo")
-            pair(4, "xc", "mc")
-            score("pkO", "mo", 4, 64, False, False)
-            fused("mc", "offc", 0, 4)
-            score("pkO", "mo", 8, 128, False, True)
-            pair(5, "xc", "mc")
-            copy_s(T.kO[:], T.pkO[:, 0:192], ["pkO"], ["kO"])
-            bias("pkA", 0, 128, 0)
-            score("pkA", "mc", 0, 0, False, False)
-            fused("mc", "offc", 4, 8)
-        score("pkA", "mc", 4, 64, False, True)
-        copy_s(T.kC[:, 0:128], T.pkA[:, 0:128], ["pkA"], ["kCa"])
-        copy_s(T.Dt[:, 0:128], T[dcur][:, 0:128], [dcur], ["Dt"])
-        bias("pkB", 128, 192, 64)
-        score("pkB", "mc", 8, 0, True, True)
-        mm(T.pM1[:, 0:192], T.idn[:], T[dcur][:], True, False, ["idn", dcur], ["pM1"])
-        scan(T.sO[:], T.rst[:], T.kO[:], A_.max, ["rst", "kO"], ["sO"])
-        ts(T.hiO[:, 0:12], T.sO[:, 15:192:16], 0xFFF000, A_.bitwise_and, ["sO"], ["hiO"])
-        tt(T.OHO[:], T.sO[:].indirect(T.rep15[:]), T.kO[:], A_.is_equal, ["sO", "rep15", "kO"], ["OHO"])
-        tt(T.thr[:, 0:12], T.pkO[:, 192:204], T.hiO[:, 0:12], A_.subtract, ["pkO", "hiO"], ["thr"])
-        tt(T.wO[:], T.OHO[:], T.pZ[:, 0:192], A_.mult, ["OHO", "pZ"], ["wO"])
-        scan(T.so[:], T.rst[:], T.wO[:], A_.add, ["rst", "wO"], ["so"])
-        tt(T.Q[:], T.so[:].indirect(T.rep15[:]), X(c_in), A_.subtract, ["so", "rep15", c_in], ["Q"])
-        copy_s(T.pZ[:, 192:384], T.Q[:], ["Q"], ["pZ"])
-        scan(T.sP[:, 0:128], T.rst[:, 0:128], T.kC[:, 0:128], A_.max, ["rst", "kCa"], ["sPa"])
-        scan(T.sP[:, 128:192], T.rst[:, 128:192], T.pkB[:, 0:64], A_.max, ["rst", "pkB"], ["sPb"])
-        copy_s(T.kC[:, 128:192], T.pkB[:, 0:64], ["pkB"], ["kCb"])
-        tt(T.eff[:, 0:12], T.sP[:, 15:192:16], T.thr[:, 0:12], A_.max, ["sPa", "sPb", "thr"], ["eff"])
-        ts(T.lo[:, 0:12], T.eff[:, 0:12], 4095, A_.bitwise_and, ["eff"], ["lo"])
+            tt(T.gn[:], X(c_in), T.kC[:, 192:384], A_.not_equal, [c_in, "kC"], ["gn"])
+            mm(T.kC[:, 192:384], T.idg[:], T.gn[:], True, True, ["idg", "gn"], ["kC"])
+            pack_in(t)
+            tt(T.am[:], T.mf[:], T.kC[:, 192:384], A_.add, ["mf", "kC"], ["am"])
+            add_k("offm", "am")
+            mid = (VA + 192) // 8 * 4
+            gather(False, "xa", "offm", VA, mid, T.xph[:])
+            gather(False, "xa", "offm", mid, 192, T.xph[:])
+            gather(True, "xa", "offm", 0, VA, T.xph[:])
+            columns(T.Cp[:, 0:192], "Cp", "ci", "cf")
+            add_k("offc", "cf")
+            gather(False, "xc", "offc", 12 * RC, 192)
+            if XE < XF:
+                gather(False, "xo", "offo", XE, XF)
+            for a, b in ((0, VA), (VA, mid), (mid, 192)):
+                scan(lanes("sa", a, b), T.rsa[:, 0:16 * (b - a)], lanes("xa", a, b), A_.add, ["rsa"] + part("xa", a, b),
+                     ["sa%d" % a])
+            SA = ["sa0", "sa%d" % VA, "sa%d" % mid]
+            ts2(T.Z[:, 192:384], T.sa[:, 15:3072:16], 1.5 * 2.0 ** 23, 1.5 * 2.0 ** 23, A_.add, A_.subtract, SA, ["Z"])
+            tt(T.up[:], T.sa[:, 15:3072:16], T.Z[:, 192:384], A_.not_equal, SA + ["Z"], ["up"])
+            minus_x("xo", *So[0])
+            minus_x("xo", *So[1])
+            mm(Dp, T.id16[:], T.up[:], False, True, ["id16", "up"], ["Dp"])
+            ts2(T.DB[:], Dp, 1.0, 255.0, A_.max, A_.min, ["Dp"], ["DB"])
+            twice(copy_v, RP)
+            spread(act, range(0, KR), RC)
+            spread(copy_v, range(KR, 16), RC)
+            o1, c1, c2, c3 = CUTR
+            done = [RP] + [b // 12 for a, b in So]
+            plus_d(*So[0])
+            plus_d(*So[1])
+            bias_o()
+            relu("mo", *So[0])
+            fused("mo", "offo", 0, o1)
+            for j in range(1, len(So)):
+                if j + 1 < len(So):
+                    minus("xo", *So[j + 1])
+                else:
+                    score("kO", "mo", 0, o1, True)
+                    minus("xc", *Sc[0])
+                relu("mo", *So[j])
+                score("kO", "mo", done[j - 1], done[j], False)
+            fused("mo", "offo", o1, RP)
+            act(T.DA[:], T.DB[:].indirect(T.toA[:, 0:12]), ["DB", "toA"], ["DA"])
+            score("kO", "mo", done[-2], 16, False)
+            score("kO", "mo", o1, RP, True, True)
+            fused("mc", "offc", 0, c1)
+            for j in range(len(Sc)):
+                if j + 1 < len(Sc):
+                    minus("xc", *Sc[j + 1])
+                relu("mc", *Sc[j])
+            start_d()
+            pool_choice()
+            pool_hot()
+            bias_c()
+            for r in range(RP, RC):
+                mm(T.kC[:, 0:192], E("NE", r), lanes("dx", 12 * r, 12 * r + 12), False, False, ["NE"] + DX, ["kC"])
+            score("kC", "mc", RC, 16, True)
+            fused("mc", "offc", c1, c2)
+            score("kC", "mc", 0, c1, False)
+            pool_card(t)
+            thr_c()
+            act(T.Q[:], T.kO[:, 192:384], ["kO"], ["Q"])
+            fused("mc", "offc", c2, c3)
+            score("kC", "mc", c1, c3, False)
+            fused("mc", "offc", c3, RC)
+            score("kC", "mc", c3, RC, False, True)
+        scan(T.sP[:], T.rst[:], T.kC[:, 0:192], A_.mult, ["rst", "kC"], ["sP"])
+        ts(T.lo[:, 0:12], T.sP[:, 15:192:16], 4095, A_.bitwise_and, ["sP"], ["lo"])
+        base = "baseR" if back else "baseN"
+        ts2(T.loc[:, 0:12], T.lo[:, 0:12], -1.0, T[base][:, 0:1], A_.mult, A_.add, ["lo", base], ["loc"])
         if not last:
-            tt(T.sw[:, 0:12], T.eff[:, 0:12], T.thr[:, 0:12], A_.is_gt, ["eff", "thr"], ["sw"])
-            mm(T.pM2[:, 16:28], T.ones[:, 0:128], T.sw[:, 0:12], True, True, ["ones", "sw"], ["pM2"])
-        copy_v(T.offs[:, 0:12], T.lo[:, 0:12], ["lo"], ["offs"])
-        tt(T.ind[:], T.mc[:].indirect(T.offs[:, 0:12]), T.Dt[:], A_.is_equal,
-           blk("mc", 0, 12) + ["mc_end", "offs", "Dt", "Dt0"], ["ind"])
-        mm(T.pM1[:, 0:192], T.id4[:], T.ind[:], False, True, ["id4", "ind"], ["pM1"])
-        tt(T.OHP[:], T.eff[:, 0:12].indirect(T.rep[:]), T.kC[:], A_.is_equal, ["eff", "rep", "kCa", "kCb"], ["OHP"])
+            ts(T.sw[:, 0:12], T.lo[:, 0:12], 0.0, A_.is_gt, ["lo"], ["sw"])
+            mm(T.pd1[:, 0, 0:12], T.ones[:, 0:128], T.sw[:, 0:12], True, True, ["ones", "sw"], ["pd1"])
+            act(T.junk[:, 0:12], T.pd1[:, 0, 0:12], ["pd1"], ["cnt", "junk"], F_.Identity, bias=344.0, accum_out=T.cnt[:])
+            act(T.nkt[:], T.cnt[:], ["cnt"], ["nkt"], F_.Identity, scale=-1.0, bias=15.5)
+            act(T.K[:], T.cnt[:], ["cnt", "nkt"], ["K"], F_.Identity, bias=T.nkt[:, 0:1])
 
-        def pack_out():
-            tt(T.pkA[:, 192:384], T.OHP[:], T.pZ[:, 192:384], A_.mult, ["OHP", "pZ"], ["pkA"])
-            tt(X(c_out), X(c_in), T.pkA[:, 192:384], A_.add, [c_in, "pkA"], [c_out])
-            return 0 if last else send_pack(t)
-        if t >= 3:
-            left += pack_out()
-        if last:
-            ts(T.ydf[:], T.pM1[:, 0:192], 1.0, A_.max, ["pM1"], ["ydf"])
-            dma("y", T.yd[:], T.ydf[:], "s_yd", ["ydf"], [])
-        else:
-            nxt = "D1" if t % 2 == 0 else "D0"
-            ts(T[nxt][:], T.pM1[:, 0:192], 1.0, A_.max, ["pM1"], [nxt])
-            dcur = nxt
-            V(lambda: v.tensor_reduce(T.kc[:], T.pM2[:, 16:28], AxisListType.X, A_.add), ["pM2"], ["kc"])
-            emit_e(dcur)
-            if t + 1 < 4:
-                emit_dx(dcur, ())
+        def demands():
+            tt(T.ind[:], T.mc[:].indirect(T.loc[:, 0:12]), T.DA[:], A_.is_ge,
+               part("mc", 0, 192) + part("xc", 0, 192) + ["mc_end3072", "mc_end%d" % (MW - 16), "loc", "DA"], ["ind"])
+            tt(T.tv[:], T.ind[:], nu, A_.mult, ["ind", "Cp"], ["tv"])
+            mm(T.Z[:, 0:192], T.W8[:], T.ind[:], False, False, ["W8", "ind"], ["Z"])
+            mm(Dp, T.id4[:], T.ind[:], False, False, ["id4", "ind"], ["Dp"])
+            mm(Dp, T.idn[:], T.tv[:], False, True, ["idn", "tv"], ["Dp"])
+            mm(T.Z[:, 0:192], T.W2[:], T.tv[:], False, True, ["W2", "tv"], ["Z"])
+            if last:
+                act(T.ydf[:], Dp, ["Dp"], ["ydf"])
+                dma("y", T.yd[:], T.ydf[:], "s_yd", ["ydf"], [])
+            else:
+                act(T.DA[:], Dp, ["Dp"], ["DA"])
+
+        def cards():
+            tt(T.tC[:], T.Iw[:].indirect(T.loc[:, 0:12]), T.Q[:], A_.mult,
+               ["Iw0", "Iw", "Iw_c0", "Iw_c1", "Iw_end3072", "Iw_end%d" % (MW - 16), "loc", "Q"], ["tC"])
+            mm(T.pd0[:, 0:12, :], T.BOf[:], T.tC[:], True, True, ["BOf", "tC"], ["pd0"])
+            tt(X(c_out), T.Cp[:, 0:192], T.tC[:], A_.add, ["Cp", "tC"], [c_out])
+            if last:
+                dma("s", T.yc[:], X(c_out), "s_yc", [c_out], [])
+                return 0
+            return send_pack(t)
+
+        def pool_out(out, name):
+            tt(T.OO[:], T.OHO[:], T.pd0[:, 0:12, :], A_.mult, ["OHO", "pd0"], ["OO"])
+            tt(out, T.Op[:, 0:192], T.OO[:], A_.subtract, ["Op", "OO"], [name])
         if t < 3:
-            left += pack_out()
-        scan(T.ds[:], T.rst[:], T.pkA[:, 192:384], A_.add, ["rst", "pkA"], ["ds"])
-        if not last:
-            ts2(T.kq[:], T.kc[:], 1.0 / 32, -0.5 + 1.0 / 64, A_.mult, A_.add, ["kc"], ["kq"])
-        tt(T.OO[:], T.ds[:].indirect(T.rep15[:]), T.OHO[:], A_.mult, ["ds", "rep15", "OHO"], ["OO"])
-        if not last:
-            ts2(T.K[:], T.kq[:], -32.0, T.kc[:, 0:1], A_.mult, A_.add, ["kq", "kc"], ["K"])
-        tt(X(onx), T.pZ[:, 0:192], T.OO[:], A_.subtract, ["pZ", "OO"], [onx])
-        if not last:
+            demands()
+            left += cards()
+            demands_to_dx(True)
             emit_v()
-        if last:
-            seat_out(c_out, "ycf", "cv1", "cv2", T.yc, "s_yc", "y", copy_s)
-            seat_out(onx, "yof", "cv3", "cv4", T.yo, "s_yo", "y", copy_v)
-        if 1 <= t < NV - 1:
-            rc = "rec%d" % t
-            copy_v(T.rec[:, 24 * t:24 * t + 12], T.lo[:, 0:12], ["lo"], [rc])
-            tt(T.rec[:, 24 * t + 12:24 * t + 24], T.so[:, 15:192:16], T.ds[:, 15:192:16], A_.subtract, ["so", "ds"], [rc])
-            left += send_rec(t)
-        ocur = onx
+            pool_out(T.Op[:, 0:192], "Op")
+        elif not last:
+            left += cards()
+            demands()
+            demands_to_dx(False)
+            mm(T.kC[:, 192:384], T.idf[:], X("cout%d" % (t - 3)), True, True, ["idf", "cout%d" % (t - 3)], ["kC"])
+            pool_out(T.Op[:, 0:192], "Op")
+            emit_v()
+        else:
+            cards()
+            demands()
+            pool_out(T.yof[:], "yof")
+            dma("y", T.yo[:], T.yof[:], "s_yo", ["yof"], [])
+        if not last:
+            columns(T.Op[:, 0:192], "Op", "pi", "pf")
+            add_k("offo", "pf")
+            if t < 3:
+                spread(copy_v, range(KS + KG, 16), RN)
     for sem in ("sv", "ss", "sp", "sg"):
         need("g", sem, count[sem])
-    for sem in ("l_po", "l_dm", "l_pk", "l_wt", "l_xt", "s_yc", "s_yo", "s_yd"):
+    for sem in ("l_po", "l_dm", "l_pk", "l_wt", "l_xt", "l_w2", "l_p1", "l_p2", "l_i0", "l_i1", "s_yc", "s_yo", "s_yd"):
         need("g", sem, 16)
+    need("g", "l_ph", 128)
     g.wait_ge(T.sem.ls, left)

@@ -7,11 +7,13 @@ F_ = ActivationFunctionType
 WT = 4096 + 32
 RN = 10
 RP, RC = 7, 11
-VA = 80
-CUTN, CUTR = (4, 7, 3, 5, 8), (4, 4, 6, 9)
-KS, KG = 9, 0
-XE, XF = 144, 168
-KR = 5
+VA = 72
+CUTN, CUTR = (4, 5, 8, 1, 5, 9), (4, 4, 6, 10)
+SN = (148, 180)
+KS, KG = 8, 2
+XE, XF = 140, 192
+KH = 2
+KR = 3
 ZB = 129 * 2048
 
 
@@ -32,7 +34,9 @@ SCRATCH.update(_sb("bfloat16", "d2", w=384))
 SCRATCH.update(_sb("float32", "baseN", "baseR", w=1))
 SCRATCH.update(_sb("bfloat16", "rsa", w=16 * VA))
 SCRATCH.update(_sb("bfloat16", "E", "NE", w=144))
-SCRATCH.update(_sb("bfloat16", "idn", "nid", "id4", "id16", "idg", "neg", "BO", "W2", "W8", w=128))
+SCRATCH.update(_sb("bfloat16", "idn", "nid", "id4", "id16", "BO", "W2", "W8", w=128))
+SCRATCH.update(_sb("bfloat16", "neg", "rsb"))
+SCRATCH.update(_sb("float32", "q12", w=1))
 SCRATCH.update(_sb("float32", "idf", "nidf", "BOf", w=128))
 SCRATCH.update(_sb("bfloat16", "ones", "rst", "gn", "ind", "tv", "up", "hq", "OHO", "DA", "DB"))
 SCRATCH.update(_sb("int32", "pki", "poi", "dmi", "pi", "pf", "ci", "cf", "mi", "mf", "sO", "sP"))
@@ -170,8 +174,6 @@ def rank_program(g, core, T, topo):
     dma("y", T.xtw[:, 4096:WT], T.xt[:, 0:32], "l_w2", [], ["xt_wrap"])
     dma("y", T.pki[:], T.pk[:], "l_pk", [], ["pki"])
     XT = ["xtw", "xt_wrap"]
-    dma("y", T.xph[:, 0:WT], T.xtw[:], "l_p1", XT, ["xph_a"])
-    dma("y", T.xph[:, WT:2 * WT], T.xtw[:], "l_p2", XT, ["xph_b"])
     fill(T.ones[:], 1.0, ["ones"])
     iota(T.iD[:], [[-1, 16]], 128, 1, ["iD"])
     iota(T.iC[:], [[1, 16]], 0, 0, ["iC"])
@@ -188,56 +190,51 @@ def rank_program(g, core, T, topo):
     iota(T.crow[:], [[-1, 192]], 0, 0, ["crow"], True)
     fill(T.K[:], 0.0, ["K"])
     ts(T.iE[:], T.iD[:], 15, A_.bitwise_and, ["iD"], ["iE"])
+    fill(T.rst[:], 1.0, ["rst"])
     copy_v(T.qf[:], T.iE[:, 0:1], ["iE"], ["qf"])
+    ts(T.Iw[:, 0:16], T.iE[:], 0.0, A_.is_equal, ["iE"], ["Iw0"])
+    fill(T.rst[:, 0:192:16], 0.0, ["rst"])
     ts2(T.iF[:], T.iC[:], 16.0, T.qf[:, 0:1], A_.mult, A_.add, ["iC", "qf"], ["iF"])
+    ts2(T.rb[:], T.qf[:], -192.0, -1024.0, A_.mult, A_.add, ["qf"], ["rb"])
+    copy_v(T.rep[:], T.iC[:], ["iC"], ["rep"])
     ts2(T.iG[:], T.iF[:], -5.5, 1.0 / 12, A_.add, A_.mult, ["iF"], ["iG"])
     ts(T.iH[:], T.iF[:], 16.0, A_.mult, ["iF"], ["iH"])
+    ts(T.q12[:], T.qf[:], 12.0, A_.mult, ["qf"], ["q12"])
     ts(T.iG[:], T.iG[:], -191.0, A_.mult, ["iG"], ["iG"])
-    ts(T.wtf[:], T.wti[:], 2.0, A_.mult, ["wti"], ["wtf"])
+    for nm, rv in (("baseN", RN), ("baseR", RC)):
+        ts2(T[nm][:], T.qf[:], rv - 0.5, float(XC), A_.is_gt, A_.mult, ["qf"], [nm])
     tt(T.iH[:], T.iH[:], T.iG[:], A_.add, ["iH", "iG"], ["iH"])
-    copy_v(T.DA[:], T.dmi[:], ["dmi"], ["DA"])
+    for nm in ("baseN", "baseR"):
+        ts(T[nm][:], T[nm][:], 3072.0, A_.add, [nm], [nm])
     copy_v(T.toB[:], T.iH[:], ["iH"], ["toB"])
+    ts(T.toA[:], T.iC[:], T.q12[:, 0:1], A_.add, ["iC", "q12"], ["toA"])
+    ts(T.wtf[:], T.wti[:], 2.0, A_.mult, ["wti"], ["wtf"])
+    copy_v(T.DA[:], T.dmi[:], ["dmi"], ["DA"])
     ts(T.W2[:], T.BO[:], T.wtf[:, 0:1], A_.mult, ["BO", "wtf"], ["W2"])
-    act(T.idf[:], T.idn[:], ["idn"], ["idf"])
+    for nm, src, c in (("idf", "idn", 1.0), ("nid", "idn", -1.0), ("nidf", "idn", -1.0), ("id4", "idn", -4.0),
+                       ("id16", "idn", 16.0), ("BOf", "BO", 1.0)):
+        act(T[nm][:], T[src][:], [src], [nm], scale=c)
     copy_v(T.O0[:], T.poi[:], ["poi"], ["O0"])
+    fill(T.rsb[:], 0.0, ["rsb"])
+    fill(T.neg[:], -0.0625, ["neg"])
+    fill(T.rsb[:, 0:192:16], -2.0 ** 26, ["rsb"])
+    for a in (3072, XC + 3072):
+        fill(T.Iw[:, a:a + 16], 0.0, ["Iw_end%d" % a])
+        fill(T.mc[:, a:a + 16], -1.0, ["mc_end%d" % a])
+    w = 16
+    while w < 1536:
+        d = min(w, 1536 - w)
+        select(T.Iw[:, w:w + d], T.Iw[:, 0:d], [[0, d]], A_.is_ge, 0.0, 0, 0, ["Iw0", "Iw"], ["Iw"])
+        w += d
+    for i, (a, b) in enumerate(((1536, 3072), (3088, MW - 16))):
+        dma("y", T.Iw[:, a:b], T.Iw[:, 0:b - a], "l_i%d" % i, ["Iw0", "Iw"], ["Iw_c%d" % i])
+    dma("y", T.xph[:, 0:WT], T.xtw[:], "l_p1", XT, ["xph_a"])
+    dma("y", T.xph[:, WT:2 * WT], T.xtw[:], "l_p2", XT, ["xph_b"])
+    select(T.rsa[:], T.Iw[:, 0:16 * VA], [[0, VA], [1, 16]], A_.is_gt, 0.0, -16, 0, ["Iw0", "Iw"], ["rsa"])
+    select(T.rsa[:, 0:16 * VA:16], T.rsa[:, 0:16 * VA:16], [[0, VA]], A_.is_gt, -2.0 ** 26, 0, 0, ["rsa"], ["rsa"])
 
-    def constants_1():
-        ts(T.nid[:], T.idn[:], -1.0, A_.mult, ["idn"], ["nid"])
-        ts(T.NE[:], T.E[:], -1.0, A_.mult, ["E"], ["NE"])
-        for nm, rv in (("baseN", RN), ("baseR", RC)):
-            ts2(T[nm][:], T.qf[:], rv - 0.5, float(XC), A_.is_gt, A_.mult, ["qf"], [nm])
-            ts(T[nm][:], T[nm][:], 3072.0, A_.add, [nm], [nm])
-        copy_v(X("cin0"), T.pki[:], ["pki"], ["cin0"])
-        fill(T.rsa[:], 0.0, ["rsa"])
-        copy_v(T.rep[:], T.iC[:], ["iC"], ["rep"])
-        fill(T.rsa[:, 0:16 * VA:16], -2.0 ** 26, ["rsa"])
-        ts(T.Iw[:, 0:16], T.iE[:], 0.0, A_.is_equal, ["iE"], ["Iw0"])
-        ts2(T.rb[:], T.qf[:], -192.0, -1024.0, A_.mult, A_.add, ["qf"], ["rb"])
-        for a in (3072, XC + 3072):
-            fill(T.Iw[:, a:a + 16], 0.0, ["Iw_end%d" % a])
-            fill(T.mc[:, a:a + 16], -1.0, ["mc_end%d" % a])
-        fill(T.rst[:], 1.0, ["rst"])
-        ts(T.id4[:], T.idn[:], -4.0, A_.mult, ["idn"], ["id4"])
-        fill(T.rst[:, 0:192:16], 0.0, ["rst"])
-        ts(T.W8[:], T.W2[:], -4.0, A_.mult, ["W2"], ["W8"])
-        w = 16
-        while w < 1536:
-            d = min(w, 1536 - w)
-            select(T.Iw[:, w:w + d], T.Iw[:, 0:d], [[0, d]], A_.is_ge, 0.0, 0, 0, ["Iw0", "Iw"], ["Iw"])
-            w += d
-        for i, (a, b) in enumerate(((1536, 3072), (3088, MW - 16))):
-            dma("y", T.Iw[:, a:b], T.Iw[:, 0:b - a], "l_i%d" % i, ["Iw0", "Iw"], ["Iw_c%d" % i])
-        if RN > RC:
-            fill(T.mc[:, XC + 192 * RC:XC + 192 * RN], 0.0, part("xc", 12 * RC, 12 * RN))
-        act(T.nidf[:], T.idn[:], ["idn"], ["nidf"], scale=-1.0)
-        act(T.BOf[:], T.BO[:], ["BO"], ["BOf"])
-
-    def constants_2():
-        fill(T.neg[:], -0.0625, ["neg"])
-        ts(T.id16[:], T.idn[:], 16.0, A_.mult, ["idn"], ["id16"])
-        ts(T.idg[:], T.idn[:], float(WT), A_.mult, ["idn"], ["idg"])
-        ts(T.wtf[:], T.qf[:], 12.0, A_.mult, ["qf"], ["wtf"])
-        ts(T.toA[:], T.iC[:], T.wtf[:, 0:1], A_.add, ["iC", "wtf"], ["toA"])
+    if RN > RC:
+        fill(T.mc[:, XC + 192 * RC:XC + 192 * RN], 0.0, part("xc", 12 * RC, 12 * RN))
 
     def return_tables(half):
         nm, c, piece = (("cs", -127.5, "xph_a"), ("cg", -128.0, "xph_b"))[half]
@@ -337,24 +334,31 @@ def rank_program(g, core, T, topo):
         start_z(False)
 
     def pack_in(t):
-        if t > 0:
+        if 0 < t < 4:
             arrived("cin%d" % t, "arr%d" % t, 8)
         mm(T.Cp[:, 0:192], T.idf[:], X("cin%d" % t), True, True, ["idf", "cin%d" % t], ["Cp"])
 
     def pool_choice():
-        scan(T.sO[:], T.rsa[:, 0:192], T.kO[:, 0:192], A_.add, ["rsa", "kO"], ["sO"])
+        scan(T.sO[:], T.rsb[:], T.kO[:, 0:192], A_.add, ["rsb", "kO"], ["sO"])
         ts(T.jo[:, 0:12], T.sO[:, 15:192:16], 15, A_.bitwise_and, ["sO"], ["jo"])
         ts2(T.hi[:, 0:12], T.sO[:, 15:192:16], 1.5 * 2.0 ** 35, 1.5 * 2.0 ** 35, A_.add, A_.subtract, ["sO"], ["hi"])
         ts2(T.ju[:, 0:12], T.jo[:, 0:12], -1.0, 15.0, A_.mult, A_.add, ["jo"], ["ju"])
 
     def pool_hot():
         act(T.OHO[:], T.Iw[:, 0:16].indirect(T.ju[:, 0:12]), ["Iw0", "ju"], ["OHO"])
+
+    def pool_least():
         act(T.hrep[:], T.hi[:, 0:12].indirect(T.rep[:, 0:12]), ["hi", "rep", "rb"], ["hrep"], F_.Identity, bias=T.rb[:, 0:1])
 
-    def pool_card(t):
-        tt(T.wO[:], T.OHO[:], T.Op[:, 0:192], A_.mult, ["OHO", "Op"], ["wO"])
+    def less_pack(t):
         mm(T.kO[:, 192:384], T.nidf[:], X("cin%d" % t), True, False, ["nidf", "cin%d" % t], ["kO"])
+
+    def pool_mask():
+        tt(T.wO[:], T.OHO[:], T.Op[:, 0:192], A_.mult, ["OHO", "Op"], ["wO"])
+
+    def pool_card():
         mm(T.kO[:, 192:384], T.BOf[:], T.wO[:], False, True, ["BOf", "wO"], ["kO"])
+        act(T.Q[:], T.kO[:, 192:384], ["kO"], ["Q"])
 
     def bias_o():
         mm(T.kO[:, 0:192], T.ones[0:1, 0:128], T.orow[:], True, False, ["ones", "orow"], ["kO"])
@@ -365,10 +369,6 @@ def rank_program(g, core, T, topo):
     def thr_c():
         mm(T.kC[:, 0:192], T.idf[:], T.hrep[:], False, False, ["idf", "hrep"], ["kC"])
 
-    def thirds(a, b):
-        w = (b - a + 11) // 12 * 4
-        return [(a, a + w), (a + w, a + 2 * w), (a + 2 * w, b)]
-
     def runs(a, b):
         k = (b - a + 31) // 32
         w = ((b - a + k - 1) // k + 3) // 4 * 4
@@ -378,37 +378,68 @@ def rank_program(g, core, T, topo):
         act(T.DB[:], T.DA[:].indirect(T.toB[:, 0:12]), ["DA", "toB"], ["DB"])
         if full:
             spread(act, range(0, KS), RN)
-            spread(copy_g, range(KS, KS + KG), RN)
-            twice(act, RN)
+            spread(copy_g if full > 1 else act, range(KS, KS + KG), RN)
 
     left = 0
     start_z(True)
     mm(T.Op[:, 0:192], T.idf[:], T.O0[:], True, True, ["idf", "O0"], ["Op"])
     demands_to_dx(True)
-    emit_v()
-    columns(T.Op[:, 0:192], "Op", "pi", "pf")
-    add_k("offo", "pf")
-    spread(copy_v, range(KS + KG, 16), RN)
+
+    def weave(chain, fill_ins):
+        fill_ins = list(fill_ins)
+        for step in chain:
+            step()
+            if fill_ins:
+                fill_ins.pop(0)()
+        for step in fill_ins:
+            step()
+
+    def copies(ks, rv):
+        return [lambda k=k: spread(copy_v, [k], rv) for k in ks]
+
+    def times(a, cards, bank):
+        return lambda: tt(T[a][:], cards, T.vp[:], A_.mult, ["vp", bank], [a])
+
+    def shift(b, a):
+        return lambda: ts2(T[b][:], T[a][:], 5, 4095, A_.arith_shift_right, A_.bitwise_and, [a], [b])
+
+    def plus_k(off, b):
+        return lambda: add_k(off, b)
+
+    def round_z():
+        ts(T.hq[:], T.Z[:, 0:192], -1056.0, A_.add, ["Z"], ["hq"])
+
+    def make_v():
+        tt(T.vp[:], T.Z[:, 0:192], T.hq[:], A_.subtract, ["Z", "hq"], ["vp"])
+
+    pool_list = [times("pi", T.Op[:, 0:192], "Op"), shift("pf", "pi"), plus_k("offo", "pf")]
+    pack_list = [times("ci", T.Cp[:, 0:192], "Cp"), shift("cf", "ci"), plus_k("offc", "cf")]
+    weave([round_z, make_v] + pool_list,
+          [lambda: copy_v(X("cin0"), T.pki[:], ["pki"], ["cin0"]), lambda: ts(T.NE[:], T.E[:], -1.0, A_.mult, ["E"], ["NE"]),
+           lambda: ts(T.W8[:], T.W2[:], -4.0, A_.mult, ["W2"], ["W8"])] + copies(range(KS + KG, 16), RN))
     for t in range(NV):
         back = t >= 4
         last = t == NV - 1
         c_in, c_out, mback = "cin%d" % t, "cout%d" % t, "cout%d" % (t - 4)
         if not back:
             rv = RN
-            S = thirds(12 * rv, 192)
+            S = list(zip((12 * rv,) + SN, SN + (192,)))
             done = [rv] + [b // 12 for a, b in S]
-            o1, o2, c1, c2, c3 = CUTN
-            if t == 0:
-                constants_1()
+            o0, o1, o2, c1, c2, c3 = CUTN
             gather(False, "xo", "offo", *S[0])
-            fused("mo", "offo", 0, o1)
+            twice(act, RN)
+            fused("mo", "offo", 0, o0)
             gather(False, "xo", "offo", *S[1])
             bias_o()
+            pack_in(t)
             minus("xo", *S[0])
             relu("mo", *S[0])
             minus("xo", *S[1])
-            pack_in(t)
+            pack_list[0]()
+            fused("mo", "offo", o0, o1)
+            pack_list[1]()
             fused("mo", "offo", o1, o2)
+            pack_list[2]()
             score("kO", "mo", 0, o1, True)
             score("kO", "mo", done[0], done[1], False)
             gather(False, "xo", "offo", *S[2])
@@ -418,66 +449,65 @@ def rank_program(g, core, T, topo):
             if t in (1, 2):
                 need("g", "arr%d" % t, 8)
                 return_tables(t - 1)
-            columns(T.Cp[:, 0:192], "Cp", "ci", "cf")
-            add_k("offc", "cf")
             score("kO", "mo", o1, o2, True)
             score("kO", "mo", done[1], done[3], False)
             start_d()
             fused("mo", "offo", o2, rv)
             gather(False, "xc", "offc", *S[0])
-            minus("xc", *S[0])
             score("kO", "mo", o2, rv, True, True)
+            minus("xc", *S[0])
             fused("mc", "offc", 0, c1)
             gather(False, "xc", "offc", *S[1])
-            relu("mc", *S[0])
-            minus("xc", *S[1])
-            if t == 1:
-                constants_2()
             pool_choice()
             bias_c()
-            score("kC", "mc", done[0], done[1], True)
             score("kC", "mc", 0, c1, False)
+            less_pack(t)
+            minus("xc", *S[1])
+            pool_least()
+            relu("mc", *S[0])
+            thr_c()
             fused("mc", "offc", c1, c2)
             gather(False, "xc", "offc", *S[2])
-            pool_hot()
+            score("kC", "mc", done[0], done[1], True)
+            score("kC", "mc", c1, c2, False)
             minus("xc", *S[2])
-            pool_card(t)
-            thr_c()
             relu("mc", *S[1])
+            pool_hot()
             relu("mc", *S[2])
             fused("mc", "offc", c2, c3)
-            score("kC", "mc", c1, c2, False)
-            act(T.Q[:], T.kO[:, 192:384], ["kO"], ["Q"])
-            score("kC", "mc", done[1], done[3], True)
+            score("kC", "mc", done[1], done[2], True)
             fused("mc", "offc", c3, rv)
+            pool_mask()
             score("kC", "mc", c2, c3, False)
+            score("kC", "mc", done[2], done[3], True)
             score("kC", "mc", c3, rv, False, True)
+            pool_card()
         else:
             rv = RC
             So, Sc = runs(12 * RP, 192), runs(12 * RC, 192)
             gather(False, "xo", "offo", 12 * RP, XE)
-            columns(T.kC[:, 192:384], "kC", "mi", "mf")
-            gather(True, "xo", "offo", XF, 192)
-            mm(Dp, T.neg[:], T.ones[:], True, False, ["neg", "ones"], ["Dp"])
-            mm(Dp, T.idn[:], T.DB[:], False, False, ["idn", "DB"], ["Dp"])
-            arrived(c_in, "arr%d" % t, 8)
-            tt(T.gn[:], X(c_in), T.kC[:, 192:384], A_.not_equal, [c_in, "kC"], ["gn"])
-            mm(T.kC[:, 192:384], T.idg[:], T.gn[:], True, True, ["idg", "gn"], ["kC"])
             pack_in(t)
-            tt(T.am[:], T.mf[:], T.kC[:, 192:384], A_.add, ["mf", "kC"], ["am"])
+            mm(Dp, T.ones[:, 0:128], T.neg[:], True, False, ["neg", "ones"], ["Dp"])
+            mm(Dp, T.idn[:], T.DB[:], False, False, ["idn", "DB"], ["Dp"])
+            tt(T.am[:], T.mf[:], T.pd1[:, 0:12, :], A_.add, ["mf", "pd1"], ["am"])
             add_k("offm", "am")
             mid = (VA + 192) // 8 * 4
             gather(False, "xa", "offm", VA, mid, T.xph[:])
             gather(False, "xa", "offm", mid, 192, T.xph[:])
+            pack_list[0]()
             gather(True, "xa", "offm", 0, VA, T.xph[:])
-            columns(T.Cp[:, 0:192], "Cp", "ci", "cf")
-            add_k("offc", "cf")
-            gather(False, "xc", "offc", 12 * RC, 192)
+            pack_list[1]()
             if XE < XF:
                 gather(False, "xo", "offo", XE, XF)
-            for a, b in ((0, VA), (VA, mid), (mid, 192)):
+
+            def most(a, b):
                 scan(lanes("sa", a, b), T.rsa[:, 0:16 * (b - a)], lanes("xa", a, b), A_.add, ["rsa"] + part("xa", a, b),
                      ["sa%d" % a])
+            most(VA, mid)
+            pack_list[2]()
+            most(0, VA)
+            most(mid, 192)
+            gather(False, "xc", "offc", *Sc[0])
             SA = ["sa0", "sa%d" % VA, "sa%d" % mid]
             ts2(T.Z[:, 192:384], T.sa[:, 15:3072:16], 1.5 * 2.0 ** 23, 1.5 * 2.0 ** 23, A_.add, A_.subtract, SA, ["Z"])
             tt(T.up[:], T.sa[:, 15:3072:16], T.Z[:, 192:384], A_.not_equal, SA + ["Z"], ["up"])
@@ -485,9 +515,10 @@ def rank_program(g, core, T, topo):
             minus_x("xo", *So[1])
             mm(Dp, T.id16[:], T.up[:], False, True, ["id16", "up"], ["Dp"])
             ts2(T.DB[:], Dp, 1.0, 255.0, A_.max, A_.min, ["Dp"], ["DB"])
-            twice(copy_v, RP)
+            twice(act, RP)
             spread(act, range(0, KR), RC)
-            spread(copy_v, range(KR, 16), RC)
+            spread(copy_g, range(KR, KR + KH), RC)
+            spread(copy_v, range(KR + KH, 16), RC)
             o1, c1, c2, c3 = CUTR
             done = [RP] + [b // 12 for a, b in So]
             plus_d(*So[0])
@@ -504,6 +535,7 @@ def rank_program(g, core, T, topo):
                 relu("mo", *So[j])
                 score("kO", "mo", done[j - 1], done[j], False)
             fused("mo", "offo", o1, RP)
+            gather(False, "xc", "offc", Sc[1][0], 192)
             act(T.DA[:], T.DB[:].indirect(T.toA[:, 0:12]), ["DB", "toA"], ["DA"])
             score("kO", "mo", done[-2], 16, False)
             score("kO", "mo", o1, RP, True, True)
@@ -514,6 +546,7 @@ def rank_program(g, core, T, topo):
                 relu("mc", *Sc[j])
             start_d()
             pool_choice()
+            pool_least()
             pool_hot()
             bias_c()
             for r in range(RP, RC):
@@ -521,11 +554,12 @@ def rank_program(g, core, T, topo):
             score("kC", "mc", RC, 16, True)
             fused("mc", "offc", c1, c2)
             score("kC", "mc", 0, c1, False)
-            pool_card(t)
+            less_pack(t)
             thr_c()
-            act(T.Q[:], T.kO[:, 192:384], ["kO"], ["Q"])
             fused("mc", "offc", c2, c3)
+            pool_mask()
             score("kC", "mc", c1, c3, False)
+            pool_card()
             fused("mc", "offc", c3, RC)
             score("kC", "mc", c3, RC, False, True)
         scan(T.sP[:], T.rst[:], T.kC[:, 0:192], A_.mult, ["rst", "kC"], ["sP"])
@@ -539,56 +573,77 @@ def rank_program(g, core, T, topo):
             act(T.nkt[:], T.cnt[:], ["cnt"], ["nkt"], F_.Identity, scale=-1.0, bias=15.5)
             act(T.K[:], T.cnt[:], ["cnt", "nkt"], ["K"], F_.Identity, bias=T.nkt[:, 0:1])
 
-        def demands():
+        def met():
             tt(T.ind[:], T.mc[:].indirect(T.loc[:, 0:12]), T.DA[:], A_.is_ge,
                part("mc", 0, 192) + part("xc", 0, 192) + ["mc_end3072", "mc_end%d" % (MW - 16), "loc", "DA"], ["ind"])
-            tt(T.tv[:], T.ind[:], nu, A_.mult, ["ind", "Cp"], ["tv"])
             mm(T.Z[:, 0:192], T.W8[:], T.ind[:], False, False, ["W8", "ind"], ["Z"])
             mm(Dp, T.id4[:], T.ind[:], False, False, ["id4", "ind"], ["Dp"])
-            mm(Dp, T.idn[:], T.tv[:], False, True, ["idn", "tv"], ["Dp"])
+
+        def demands():
+            tt(T.tv[:], T.ind[:], nu, A_.mult, ["ind", "Cp"], ["tv"])
             mm(T.Z[:, 0:192], T.W2[:], T.tv[:], False, True, ["W2", "tv"], ["Z"])
+            mm(Dp, T.idn[:], T.tv[:], False, True, ["idn", "tv"], ["Dp"])
             if last:
                 act(T.ydf[:], Dp, ["Dp"], ["ydf"])
                 dma("y", T.yd[:], T.ydf[:], "s_yd", ["ydf"], [])
             else:
                 act(T.DA[:], Dp, ["Dp"], ["DA"])
 
-        def cards():
+        def change():
             tt(T.tC[:], T.Iw[:].indirect(T.loc[:, 0:12]), T.Q[:], A_.mult,
                ["Iw0", "Iw", "Iw_c0", "Iw_c1", "Iw_end3072", "Iw_end%d" % (MW - 16), "loc", "Q"], ["tC"])
+
+        def spread_change():
             mm(T.pd0[:, 0:12, :], T.BOf[:], T.tC[:], True, True, ["BOf", "tC"], ["pd0"])
+
+        def pack_out():
             tt(X(c_out), T.Cp[:, 0:192], T.tC[:], A_.add, ["Cp", "tC"], [c_out])
             if last:
                 dma("s", T.yc[:], X(c_out), "s_yc", [c_out], [])
                 return 0
             return send_pack(t)
 
-        def pool_out(out, name):
+        def pool_change():
             tt(T.OO[:], T.OHO[:], T.pd0[:, 0:12, :], A_.mult, ["OHO", "pd0"], ["OO"])
+
+        def pool_out():
+            out, name = (T.yof[:], "yof") if last else (T.Op[:, 0:192], "Op")
             tt(out, T.Op[:, 0:192], T.OO[:], A_.subtract, ["Op", "OO"], [name])
         if t < 3:
+            met()
+            change()
+            spread_change()
             demands()
-            left += cards()
-            demands_to_dx(True)
-            emit_v()
-            pool_out(T.Op[:, 0:192], "Op")
+            left += pack_out()
+            demands_to_dx(2 if t else 1)
+            pool_change()
+            weave([round_z, make_v] + pool_list, [pool_out] + copies(range(KS + KG, 16), RN))
         elif not last:
-            left += cards()
+            nxt, gone = "cin%d" % (t + 1), "cout%d" % (t - 3)
+            change()
+            spread_change()
+            met()
+            left += pack_out()
             demands()
-            demands_to_dx(False)
-            mm(T.kC[:, 192:384], T.idf[:], X("cout%d" % (t - 3)), True, True, ["idf", "cout%d" % (t - 3)], ["kC"])
-            pool_out(T.Op[:, 0:192], "Op")
-            emit_v()
+            demands_to_dx(0)
+            mm(T.kC[:, 192:384], T.idf[:], X(gone), True, True, ["idf", gone], ["kC"])
+            mm(T.pd1[:, 0:12, :], T.nidf[:], X(gone), True, False, ["nidf", gone], ["pd1"])
+            pool_change()
+            arrived(nxt, "arr%d" % (t + 1), 8)
+            mm(T.pd1[:, 0:12, :], T.idf[:], X(nxt), False, True, ["idf", nxt], ["pd1"])
+            weave([round_z, make_v] + pool_list,
+                  [pool_out, lambda: None, times("mi", T.kC[:, 192:384], "kC"), shift("mf", "mi"),
+                   lambda: gather(True, "xo", "offo", XF, 192) if XF < 192 else None,
+                   lambda: ts2(T.pd1[:, 0:12, :], T.pd1[:, 0:12, :], 0.0, float(WT), A_.not_equal, A_.mult, ["pd1"], ["pd1"])])
         else:
-            cards()
+            met()
+            change()
             demands()
-            pool_out(T.yof[:], "yof")
+            spread_change()
+            pack_out()
+            pool_change()
+            pool_out()
             dma("y", T.yo[:], T.yof[:], "s_yo", ["yof"], [])
-        if not last:
-            columns(T.Op[:, 0:192], "Op", "pi", "pf")
-            add_k("offo", "pf")
-            if t < 3:
-                spread(copy_v, range(KS + KG, 16), RN)
     for sem in ("sv", "ss", "sp", "sg"):
         need("g", sem, count[sem])
     for sem in ("l_po", "l_dm", "l_pk", "l_wt", "l_xt", "l_w2", "l_p1", "l_p2", "l_i0", "l_i1", "s_yc", "s_yo", "s_yd"):

from concourse.bass import DstId, RemoteDMATransfer
from concourse.mybir import AluOpType, AxisListType, ActivationFunctionType

NV = 7
A_ = AluOpType
F_ = ActivationFunctionType
WT = 4096 + 32
RN = 10
RP, RC = 7, 11
VA = 72
CUTN, CUTR = (4, 5, 8, 1, 5, 9), (4, 4, 6, 10)
SN = (148, 180)
KS, KG = 8, 2
XE, XF = 140, 192
KH = 2
KR = 3
ZB = 129 * 2048


def _sb(dtype, *names, w=192):
    return {nm: ("sbuf", [128, w], dtype) for nm in names}


XC = 3088 - 192 * min(RN, RC)
MW = XC + 3088
SCRATCH = {"zrow": ("sbuf", [2, 192], "bfloat16"), "crow": ("sbuf", [1, 192], "bfloat16"),
           "orow": ("sbuf", [1, 192], "bfloat16")}
SCRATCH.update(_sb("bfloat16", "xtw", w=WT))
SCRATCH.update(_sb("bfloat16", "xph", w=2 * WT))
SCRATCH.update(_sb("bfloat16", "cs", "cg", w=WT // 4))
SCRATCH.update(_sb("bfloat16", "xo", "xa", "sa", "mo", "dx", w=3072))
SCRATCH.update(_sb("bfloat16", "Iw", "mc", w=MW))
SCRATCH.update(_sb("bfloat16", "d2", w=384))
SCRATCH.update(_sb("float32", "baseN", "baseR", w=1))
SCRATCH.update(_sb("bfloat16", "rsa", w=16 * VA))
SCRATCH.update(_sb("bfloat16", "E", "NE", w=144))
SCRATCH.update(_sb("bfloat16", "idn", "nid", "id4", "id16", "BO", "W2", "W8", w=128))
SCRATCH.update(_sb("bfloat16", "neg", "rsb"))
SCRATCH.update(_sb("float32", "q12", w=1))
SCRATCH.update(_sb("float32", "idf", "nidf", "BOf", w=128))
SCRATCH.update(_sb("bfloat16", "ones", "rst", "gn", "ind", "tv", "up", "hq", "OHO", "DA", "DB"))
SCRATCH.update(_sb("int32", "pki", "poi", "dmi", "pi", "pf", "ci", "cf", "mi", "mf", "sO", "sP"))
SCRATCH.update(_sb("uint16", "offo", "offc", "offm"))
SCRATCH.update(_sb("float32", "O0", "am", "vp", "wO", "Q", "tC", "OO", "hrep", "ydf", "yof"))
SCRATCH.update(_sb("int32", "wti", w=1))
SCRATCH.update(_sb("float32", "wtf", "cnt", "rb", "qf", "K", w=1))
SCRATCH.update(_sb("bfloat16", "nkt", w=1))
SCRATCH.update(_sb("int32", "iC", "iD", "iE", "iF", "iG", "iH", "jo", "lo", w=16))
SCRATCH.update(_sb("uint16", "rep", "ju", "loc", "toB", "toA", w=16))
SCRATCH.update(_sb("float32", "hi", "junk", w=16))
SCRATCH.update(_sb("bfloat16", "sw", w=16))
SCRATCH.update(_sb("float32", "cin", "cout", w=192 * NV))
PSUM = ("pd0", "pd1", "Dp", "kO", "kC", "Z", "Op", "Cp")
SCRATCH.update({nm: ("psum", [128, 512], "float32") for nm in PSUM[2:]})
SCRATCH.update({nm: ("psum", [128, 32, 16], "float32") for nm in PSUM[:2]})
SEMAPHORES = (["sv", "ss", "sp", "sg", "ls", "l_po", "l_dm", "l_pk", "l_wt", "l_xt", "l_w2", "l_p1", "l_p2", "l_ph",
               "l_i0", "l_i1", "s_yc", "s_yo", "s_yd"] + ["arr%d" % t for t in range(1, NV)])


def rank_program(g, core, T, topo):
    rank = T.rank_of(core)
    if rank is None:
        return
    n = len(T.cores)
    queue = {"v": g.vector, "s": g.scalar, "p": g.tensor, "g": g, "y": g.sync}
    own = {"v": "sv", "s": "ss", "p": "sp", "g": "sg"}
    count = {"sv": 0, "ss": 0, "sp": 0, "sg": 0}
    known = {q: {} for q in queue}
    snap = {}
    last_w, readers = {}, {}

    def need(q, sem, val):
        if known[q].get(sem, 0) >= val:
            return
        queue[q].wait_ge(T.sem[sem], val)
        known[q][sem] = val
        for k2, v2 in snap.get((sem, val), {}).items():
            if known[q].get(k2, 0) < v2:
                known[q][k2] = v2

    def order(q, reads, writes, cont=False):
        deps = {}

        def add(tok, skip_own=False):
            for sm, c in tok.items():
                if skip_own and sm == own.get(q):
                    continue
                if deps.get(sm, 0) < c:
                    deps[sm] = c
        for b in reads:
            add(last_w.get(b, {}))
            if b in PSUM:
                add(readers.get(b, {}), True)
        for b in writes:
            add(last_w.get(b, {}), q == "p" and not cont)
            add(readers.get(b, {}), True)
        for sm in sorted(deps):
            need(q, sm, deps[sm])

    def note(tok_sem, tok_val, reads, writes):
        for b in writes:
            last_w[b] = {tok_sem: tok_val}
            readers[b] = {}
        for b in reads:
            readers.setdefault(b, {})[tok_sem] = tok_val

    def op(q, fn, reads, writes, cont=False):
        order(q, reads, writes, cont)
        sem = own[q]
        fn().then_inc(T.sem[sem], 1)
        count[sem] += 1
        snap[(sem, count[sem])] = dict(known[q])
        note(sem, count[sem], reads, writes)

    def dma(q, out, in_, sem, reads, writes):
        order(q, reads, writes)
        queue[q].dma_start(out, in_).then_inc(T.sem[sem], 16)
        snap[(sem, 16)] = dict(known[q])
        note(sem, 16, reads, writes)

    def arrived(buf, sem, val):
        last_w[buf] = {sem: val}
        readers[buf] = {}

    v, s, pe = g.vector, g.scalar, g.tensor

    def X(name):
        i = int(name[-1])
        return T[name[:-1]][:, 192 * i:192 * i + 192]

    def V(fn, r, w):
        op("v", fn, r, w)

    def act(out, in_, r, w, f=F_.Copy, **kw):
        op("s", lambda: s.activation(out, in_, f, **kw), r, w)

    def copy_v(out, in_, r, w):
        V(lambda: v.tensor_copy(out, in_), r, w)

    def fill(ap, c, w):
        V(lambda: v.memset(ap, c), [], w)

    def tt(out, a, b, o, r, w):
        V(lambda: v.tensor_tensor(out, a, b, o), r, w)

    def ts(out, a, s1, o0, r, w):
        V(lambda: v.tensor_scalar(out, a, s1, None, o0), r, w)

    def ts2(out, a, s1, s2, o0, o1, r, w):
        V(lambda: v.tensor_scalar(out, a, s1, s2, o0, o1), r, w)

    def scan(out, d0, d1, o0, r, w):
        V(lambda: v.tensor_tensor_scan(out, d0, d1, 0.0, o0, A_.max), r, w)

    def mm(out, lhsT, rhs, st, sp, r, w, cont=False):
        op("p", lambda: pe.matmul(out, lhsT, rhs, st, sp), r, w, cont)

    def select(out, in_, pat, cmp, fill_, base, cm, r, w):
        op("g", lambda: g.affine_select(out, in_, pat, cmp, fill_, base, cm), r, w)

    def iota(out, pat, base, cm, w, small=False):
        if small:
            op("g", lambda: g.iota(out, pat, base, cm, allow_small_or_imprecise_dtypes=True), [], w)
        else:
            op("g", lambda: g.iota(out, pat, base, cm), [], w)

    def part(nm, a, b):
        return ["%s%d" % (nm, u) for u in range(a // 4, (b + 3) // 4)]

    dma("y", T.dmi[:], T.dm[:], "l_dm", [], ["dmi"])
    dma("s", T.xtw[:, 0:4096], T.xt[:], "l_xt", [], ["xtw"])
    dma("y", T.wti[:], T.wt[:], "l_wt", [], ["wti"])
    dma("y", T.poi[:], T.po[:], "l_po", [], ["poi"])
    dma("y", T.xtw[:, 4096:WT], T.xt[:, 0:32], "l_w2", [], ["xt_wrap"])
    dma("y", T.pki[:], T.pk[:], "l_pk", [], ["pki"])
    XT = ["xtw", "xt_wrap"]
    fill(T.ones[:], 1.0, ["ones"])
    iota(T.iD[:], [[-1, 16]], 128, 1, ["iD"])
    iota(T.iC[:], [[1, 16]], 0, 0, ["iC"])
    fill(T.E[:], 0.0, ["E"])
    fill(T.zrow[0:2, :], float(ZB), ["zrow"])
    fill(T.E[:, 15:143:16], 4096.0, ["E"])
    fill(T.zrow[0:1, :], 33.0, ["zrow"])
    select(T.BO[:], T.ones[:, 0:128], [[-16, 8], [0, 16]], A_.is_ge, 0.0, 0, 1, ["ones"], ["BO"])
    select(T.idn[:], T.ones[:, 0:128], [[-1, 128]], A_.is_equal, 0.0, 0, 1, ["ones"], ["idn"])
    select(T.BO[:], T.BO[:], [[16, 8], [0, 16]], A_.is_ge, 0.0, 15, -1, ["BO"], ["BO"])
    select(T.E[:, 15:143:16], T.E[:, 15:143:16], [[-16, 8]], A_.is_ge, 0.0, 0, 1, ["E"], ["E"])
    iota(T.orow[:], [[0, 12], [-1, 16]], 15, 0, ["orow"], True)
    select(T.E[:, 15:143:16], T.E[:, 15:143:16], [[16, 8]], A_.is_ge, 0.0, 15, -1, ["E"], ["E"])
    iota(T.crow[:], [[-1, 192]], 0, 0, ["crow"], True)
    fill(T.K[:], 0.0, ["K"])
    ts(T.iE[:], T.iD[:], 15, A_.bitwise_and, ["iD"], ["iE"])
    fill(T.rst[:], 1.0, ["rst"])
    copy_v(T.qf[:], T.iE[:, 0:1], ["iE"], ["qf"])
    ts(T.Iw[:, 0:16], T.iE[:], 0.0, A_.is_equal, ["iE"], ["Iw0"])
    fill(T.rst[:, 0:192:16], 0.0, ["rst"])
    ts2(T.iF[:], T.iC[:], 16.0, T.qf[:, 0:1], A_.mult, A_.add, ["iC", "qf"], ["iF"])
    ts2(T.rb[:], T.qf[:], -192.0, -1024.0, A_.mult, A_.add, ["qf"], ["rb"])
    copy_v(T.rep[:], T.iC[:], ["iC"], ["rep"])
    ts2(T.iG[:], T.iF[:], -5.5, 1.0 / 12, A_.add, A_.mult, ["iF"], ["iG"])
    ts(T.iH[:], T.iF[:], 16.0, A_.mult, ["iF"], ["iH"])
    ts(T.q12[:], T.qf[:], 12.0, A_.mult, ["qf"], ["q12"])
    ts(T.iG[:], T.iG[:], -191.0, A_.mult, ["iG"], ["iG"])
    for nm, rv in (("baseN", RN), ("baseR", RC)):
        ts2(T[nm][:], T.qf[:], rv - 0.5, float(XC), A_.is_gt, A_.mult, ["qf"], [nm])
    tt(T.iH[:], T.iH[:], T.iG[:], A_.add, ["iH", "iG"], ["iH"])
    for nm in ("baseN", "baseR"):
        ts(T[nm][:], T[nm][:], 3072.0, A_.add, [nm], [nm])
    copy_v(T.toB[:], T.iH[:], ["iH"], ["toB"])
    ts(T.toA[:], T.iC[:], T.q12[:, 0:1], A_.add, ["iC", "q12"], ["toA"])
    ts(T.wtf[:], T.wti[:], 2.0, A_.mult, ["wti"], ["wtf"])
    copy_v(T.DA[:], T.dmi[:], ["dmi"], ["DA"])
    ts(T.W2[:], T.BO[:], T.wtf[:, 0:1], A_.mult, ["BO", "wtf"], ["W2"])
    for nm, src, c in (("idf", "idn", 1.0), ("nid", "idn", -1.0), ("nidf", "idn", -1.0), ("id4", "idn", -4.0),
                       ("id16", "idn", 16.0), ("BOf", "BO", 1.0)):
        act(T[nm][:], T[src][:], [src], [nm], scale=c)
    copy_v(T.O0[:], T.poi[:], ["poi"], ["O0"])
    fill(T.rsb[:], 0.0, ["rsb"])
    fill(T.neg[:], -0.0625, ["neg"])
    fill(T.rsb[:, 0:192:16], -2.0 ** 26, ["rsb"])
    for a in (3072, XC + 3072):
        fill(T.Iw[:, a:a + 16], 0.0, ["Iw_end%d" % a])
        fill(T.mc[:, a:a + 16], -1.0, ["mc_end%d" % a])
    w = 16
    while w < 1536:
        d = min(w, 1536 - w)
        select(T.Iw[:, w:w + d], T.Iw[:, 0:d], [[0, d]], A_.is_ge, 0.0, 0, 0, ["Iw0", "Iw"], ["Iw"])
        w += d
    for i, (a, b) in enumerate(((1536, 3072), (3088, MW - 16))):
        dma("y", T.Iw[:, a:b], T.Iw[:, 0:b - a], "l_i%d" % i, ["Iw0", "Iw"], ["Iw_c%d" % i])
    dma("y", T.xph[:, 0:WT], T.xtw[:], "l_p1", XT, ["xph_a"])
    dma("y", T.xph[:, WT:2 * WT], T.xtw[:], "l_p2", XT, ["xph_b"])
    select(T.rsa[:], T.Iw[:, 0:16 * VA], [[0, VA], [1, 16]], A_.is_gt, 0.0, -16, 0, ["Iw0", "Iw"], ["rsa"])
    select(T.rsa[:, 0:16 * VA:16], T.rsa[:, 0:16 * VA:16], [[0, VA]], A_.is_gt, -2.0 ** 26, 0, 0, ["rsa"], ["rsa"])

    if RN > RC:
        fill(T.mc[:, XC + 192 * RC:XC + 192 * RN], 0.0, part("xc", 12 * RC, 12 * RN))

    def return_tables(half):
        nm, c, piece = (("cs", -127.5, "xph_a"), ("cg", -128.0, "xph_b"))[half]
        q = WT // 4
        select(T[nm][:], T.xtw[:, 0:q], [[0, q]], A_.is_gt, c, 0, 0, XT, [nm])
        order("g", [nm], [piece])
        for i in range(4):
            a = half * WT + i * q
            g.dma_start(T.xph[:, a:a + q], T[nm][:], accum_op=A_.add).then_inc(T.sem.l_ph, 16)
        if half:
            arrived("xph", "l_ph", 128)

    win = T.xtw[:]
    Dp = T.Dp[:, 0:192]
    nu = T.Cp[:, 192:384]
    DX = ["dx%d" % k for k in range(16)]

    def E(nm, r):
        return T[nm][:, 15 - r:143 - r]

    def start_z(stop):
        mm(T.Z[:, 0:192], T.ones[0:2, 0:128], T.zrow[:], True, False, ["ones", "zrow"], ["Z"])
        mm(T.Z[:, 0:192], T.W2[:], T.DA[:], False, stop, ["W2", "DA"], ["Z"])

    def emit_v():
        ts(T.hq[:], T.Z[:, 0:192], -1056.0, A_.add, ["Z"], ["hq"])
        tt(T.vp[:], T.Z[:, 0:192], T.hq[:], A_.subtract, ["Z", "hq"], ["vp"])

    def columns(cards, bank, a, b):
        tt(T[a][:], cards, T.vp[:], A_.mult, ["vp", bank], [a])
        ts2(T[b][:], T[a][:], 5, 4095, A_.arith_shift_right, A_.bitwise_and, [a], [b])

    def add_k(off, b):
        ts(T[off][:], T[b][:].indirect(T.toB[:, 0:12]), T.K[:, 0:1], A_.add, [b, "toB", "K"], [off])

    def copy_g(out, in_, r, w):
        select(out, in_, [[0, in_.shape[1]]], A_.is_ge, 0.0, 0, 0, r, w)

    def spread(cp, ks, rv):
        for k in ks:
            cp(T.dx[:, k:192 * rv:16], T.DB[:, 0:12 * rv], ["DB"], ["dx%d" % k])

    def twice(cp, rv):
        for k in range(2):
            cp(T.d2[:, 24 * rv + k:384:2], T.DB[:, 12 * rv:192], ["DB"], ["d2%d" % k])

    def lanes(nm, a, b):
        return T.mc[:, XC + 16 * a:XC + 16 * b] if nm == "xc" else T[nm][:, 16 * a:16 * b]

    def gather(onv, dst, off, a, b, w=None):
        i = (w or win).indirect(T[off][:, a:b])
        (copy_v if onv else act)(lanes(dst, a, b), i, (["xph"] if w is not None else XT) + [off], part(dst, a, b))

    def fused(dst, off, r0, r1):
        a, b = 12 * r0, 12 * r1
        tt(lanes(dst, a, b), win.indirect(T[off][:, a:b]), lanes("dx", a, b), A_.min, XT + [off] + DX, part(dst, a, b))

    turn = [0]

    where = {}

    def minus_x(src, a, b):
        bank = where[a] = "pd%d" % (turn[0] % 2)
        turn[0] += 1
        mm(T[bank][:, 0:b - a, :], T.nid[:], lanes(src, a, b), True, False, ["nid"] + part(src, a, b), [bank])

    def plus_d(a, b):
        bank = where[a]
        for k in range(0, 16, 2):
            mm(T[bank][:, 0:b - a, k:k + 2], T.idn[:], T.d2[:, 2 * a:2 * b], False, k == 14, ["idn", "d20", "d21"], [bank])

    def minus(src, a, b):
        minus_x(src, a, b)
        plus_d(a, b)

    def relu(dst, a, b):
        act(lanes(dst, a, b), T[where[a]][:, 0:b - a, :], [where[a]], part(dst, a, b), F_.Relu)

    def score(bank, src, r0, r1, neg, final=False):
        nm = "NE" if neg else "E"
        for r in range(r0, r1):
            mm(T[bank][:, 0:192], E(nm, r), T[src][:, 192 * r:192 * r + 192], False, final and r == r1 - 1,
               [nm] + part(src, 12 * r, 12 * r + 12), [bank])

    def send_pack(t):
        dst = T.cores[(rank + 1) % n]
        rid, pid = topo.addr(dst, core)
        need("g", *list(last_w["cout%d" % t].items())[0])
        eng = topo.engines(core, dst)[:8]
        g.remote_dma(X("cin%d" % (t + 1)), X("cout%d" % t), T.sem["arr%d" % (t + 1)], T.sem.ls, pid, rid,
                     sum(1 << e for e in eng))
        return len(eng)

    def start_d():
        act(nu, T.DA[:], ["DA"], ["Cp"], F_.Relu, scale=-1.0, bias=5.0)
        mm(Dp, T.idn[:], T.DA[:], True, False, ["idn", "DA"], ["Dp"])
        start_z(False)

    def pack_in(t):
        if 0 < t < 4:
            arrived("cin%d" % t, "arr%d" % t, 8)
        mm(T.Cp[:, 0:192], T.idf[:], X("cin%d" % t), True, True, ["idf", "cin%d" % t], ["Cp"])

    def pool_choice():
        scan(T.sO[:], T.rsb[:], T.kO[:, 0:192], A_.add, ["rsb", "kO"], ["sO"])
        ts(T.jo[:, 0:12], T.sO[:, 15:192:16], 15, A_.bitwise_and, ["sO"], ["jo"])
        ts2(T.hi[:, 0:12], T.sO[:, 15:192:16], 1.5 * 2.0 ** 35, 1.5 * 2.0 ** 35, A_.add, A_.subtract, ["sO"], ["hi"])
        ts2(T.ju[:, 0:12], T.jo[:, 0:12], -1.0, 15.0, A_.mult, A_.add, ["jo"], ["ju"])

    def pool_hot():
        act(T.OHO[:], T.Iw[:, 0:16].indirect(T.ju[:, 0:12]), ["Iw0", "ju"], ["OHO"])

    def pool_least():
        act(T.hrep[:], T.hi[:, 0:12].indirect(T.rep[:, 0:12]), ["hi", "rep", "rb"], ["hrep"], F_.Identity, bias=T.rb[:, 0:1])

    def less_pack(t):
        mm(T.kO[:, 192:384], T.nidf[:], X("cin%d" % t), True, False, ["nidf", "cin%d" % t], ["kO"])

    def pool_mask():
        tt(T.wO[:], T.OHO[:], T.Op[:, 0:192], A_.mult, ["OHO", "Op"], ["wO"])

    def pool_card():
        mm(T.kO[:, 192:384], T.BOf[:], T.wO[:], False, True, ["BOf", "wO"], ["kO"])
        act(T.Q[:], T.kO[:, 192:384], ["kO"], ["Q"])

    def bias_o():
        mm(T.kO[:, 0:192], T.ones[0:1, 0:128], T.orow[:], True, False, ["ones", "orow"], ["kO"])

    def bias_c():
        mm(T.kC[:, 0:192], T.ones[0:1, 0:128], T.crow[:], True, False, ["ones", "crow"], ["kC"])

    def thr_c():
        mm(T.kC[:, 0:192], T.idf[:], T.hrep[:], False, False, ["idf", "hrep"], ["kC"])

    def runs(a, b):
        k = (b - a + 31) // 32
        w = ((b - a + k - 1) // k + 3) // 4 * 4
        return [(x, min(x + w, b)) for x in range(a, b, w)]

    def demands_to_dx(full):
        act(T.DB[:], T.DA[:].indirect(T.toB[:, 0:12]), ["DA", "toB"], ["DB"])
        if full:
            spread(act, range(0, KS), RN)
            spread(copy_g if full > 1 else act, range(KS, KS + KG), RN)

    left = 0
    start_z(True)
    mm(T.Op[:, 0:192], T.idf[:], T.O0[:], True, True, ["idf", "O0"], ["Op"])
    demands_to_dx(True)

    def weave(chain, fill_ins):
        fill_ins = list(fill_ins)
        for step in chain:
            step()
            if fill_ins:
                fill_ins.pop(0)()
        for step in fill_ins:
            step()

    def copies(ks, rv):
        return [lambda k=k: spread(copy_v, [k], rv) for k in ks]

    def times(a, cards, bank):
        return lambda: tt(T[a][:], cards, T.vp[:], A_.mult, ["vp", bank], [a])

    def shift(b, a):
        return lambda: ts2(T[b][:], T[a][:], 5, 4095, A_.arith_shift_right, A_.bitwise_and, [a], [b])

    def plus_k(off, b):
        return lambda: add_k(off, b)

    def round_z():
        ts(T.hq[:], T.Z[:, 0:192], -1056.0, A_.add, ["Z"], ["hq"])

    def make_v():
        tt(T.vp[:], T.Z[:, 0:192], T.hq[:], A_.subtract, ["Z", "hq"], ["vp"])

    pool_list = [times("pi", T.Op[:, 0:192], "Op"), shift("pf", "pi"), plus_k("offo", "pf")]
    pack_list = [times("ci", T.Cp[:, 0:192], "Cp"), shift("cf", "ci"), plus_k("offc", "cf")]
    weave([round_z, make_v] + pool_list,
          [lambda: copy_v(X("cin0"), T.pki[:], ["pki"], ["cin0"]), lambda: ts(T.NE[:], T.E[:], -1.0, A_.mult, ["E"], ["NE"]),
           lambda: ts(T.W8[:], T.W2[:], -4.0, A_.mult, ["W2"], ["W8"])] + copies(range(KS + KG, 16), RN))
    for t in range(NV):
        back = t >= 4
        last = t == NV - 1
        c_in, c_out, mback = "cin%d" % t, "cout%d" % t, "cout%d" % (t - 4)
        if not back:
            rv = RN
            S = list(zip((12 * rv,) + SN, SN + (192,)))
            done = [rv] + [b // 12 for a, b in S]
            o0, o1, o2, c1, c2, c3 = CUTN
            gather(False, "xo", "offo", *S[0])
            twice(act, RN)
            fused("mo", "offo", 0, o0)
            gather(False, "xo", "offo", *S[1])
            bias_o()
            pack_in(t)
            minus("xo", *S[0])
            relu("mo", *S[0])
            minus("xo", *S[1])
            pack_list[0]()
            fused("mo", "offo", o0, o1)
            pack_list[1]()
            fused("mo", "offo", o1, o2)
            pack_list[2]()
            score("kO", "mo", 0, o1, True)
            score("kO", "mo", done[0], done[1], False)
            gather(False, "xo", "offo", *S[2])
            relu("mo", *S[1])
            minus("xo", *S[2])
            relu("mo", *S[2])
            if t in (1, 2):
                need("g", "arr%d" % t, 8)
                return_tables(t - 1)
            score("kO", "mo", o1, o2, True)
            score("kO", "mo", done[1], done[3], False)
            start_d()
            fused("mo", "offo", o2, rv)
            gather(False, "xc", "offc", *S[0])
            score("kO", "mo", o2, rv, True, True)
            minus("xc", *S[0])
            fused("mc", "offc", 0, c1)
            gather(False, "xc", "offc", *S[1])
            pool_choice()
            bias_c()
            score("kC", "mc", 0, c1, False)
            less_pack(t)
            minus("xc", *S[1])
            pool_least()
            relu("mc", *S[0])
            thr_c()
            fused("mc", "offc", c1, c2)
            gather(False, "xc", "offc", *S[2])
            score("kC", "mc", done[0], done[1], True)
            score("kC", "mc", c1, c2, False)
            minus("xc", *S[2])
            relu("mc", *S[1])
            pool_hot()
            relu("mc", *S[2])
            fused("mc", "offc", c2, c3)
            score("kC", "mc", done[1], done[2], True)
            fused("mc", "offc", c3, rv)
            pool_mask()
            score("kC", "mc", c2, c3, False)
            score("kC", "mc", done[2], done[3], True)
            score("kC", "mc", c3, rv, False, True)
            pool_card()
        else:
            rv = RC
            So, Sc = runs(12 * RP, 192), runs(12 * RC, 192)
            gather(False, "xo", "offo", 12 * RP, XE)
            pack_in(t)
            mm(Dp, T.ones[:, 0:128], T.neg[:], True, False, ["neg", "ones"], ["Dp"])
            mm(Dp, T.idn[:], T.DB[:], False, False, ["idn", "DB"], ["Dp"])
            tt(T.am[:], T.mf[:], T.pd1[:, 0:12, :], A_.add, ["mf", "pd1"], ["am"])
            add_k("offm", "am")
            mid = (VA + 192) // 8 * 4
            gather(False, "xa", "offm", VA, mid, T.xph[:])
            gather(False, "xa", "offm", mid, 192, T.xph[:])
            pack_list[0]()
            gather(True, "xa", "offm", 0, VA, T.xph[:])
            pack_list[1]()
            if XE < XF:
                gather(False, "xo", "offo", XE, XF)

            def most(a, b):
                scan(lanes("sa", a, b), T.rsa[:, 0:16 * (b - a)], lanes("xa", a, b), A_.add, ["rsa"] + part("xa", a, b),
                     ["sa%d" % a])
            most(VA, mid)
            pack_list[2]()
            most(0, VA)
            most(mid, 192)
            gather(False, "xc", "offc", *Sc[0])
            SA = ["sa0", "sa%d" % VA, "sa%d" % mid]
            ts2(T.Z[:, 192:384], T.sa[:, 15:3072:16], 1.5 * 2.0 ** 23, 1.5 * 2.0 ** 23, A_.add, A_.subtract, SA, ["Z"])
            tt(T.up[:], T.sa[:, 15:3072:16], T.Z[:, 192:384], A_.not_equal, SA + ["Z"], ["up"])
            minus_x("xo", *So[0])
            minus_x("xo", *So[1])
            mm(Dp, T.id16[:], T.up[:], False, True, ["id16", "up"], ["Dp"])
            ts2(T.DB[:], Dp, 1.0, 255.0, A_.max, A_.min, ["Dp"], ["DB"])
            twice(act, RP)
            spread(act, range(0, KR), RC)
            spread(copy_g, range(KR, KR + KH), RC)
            spread(copy_v, range(KR + KH, 16), RC)
            o1, c1, c2, c3 = CUTR
            done = [RP] + [b // 12 for a, b in So]
            plus_d(*So[0])
            plus_d(*So[1])
            bias_o()
            relu("mo", *So[0])
            fused("mo", "offo", 0, o1)
            for j in range(1, len(So)):
                if j + 1 < len(So):
                    minus("xo", *So[j + 1])
                else:
                    score("kO", "mo", 0, o1, True)
                    minus("xc", *Sc[0])
                relu("mo", *So[j])
                score("kO", "mo", done[j - 1], done[j], False)
            fused("mo", "offo", o1, RP)
            gather(False, "xc", "offc", Sc[1][0], 192)
            act(T.DA[:], T.DB[:].indirect(T.toA[:, 0:12]), ["DB", "toA"], ["DA"])
            score("kO", "mo", done[-2], 16, False)
            score("kO", "mo", o1, RP, True, True)
            fused("mc", "offc", 0, c1)
            for j in range(len(Sc)):
                if j + 1 < len(Sc):
                    minus("xc", *Sc[j + 1])
                relu("mc", *Sc[j])
            start_d()
            pool_choice()
            pool_least()
            pool_hot()
            bias_c()
            for r in range(RP, RC):
                mm(T.kC[:, 0:192], E("NE", r), lanes("dx", 12 * r, 12 * r + 12), False, False, ["NE"] + DX, ["kC"])
            score("kC", "mc", RC, 16, True)
            fused("mc", "offc", c1, c2)
            score("kC", "mc", 0, c1, False)
            less_pack(t)
            thr_c()
            fused("mc", "offc", c2, c3)
            pool_mask()
            score("kC", "mc", c1, c3, False)
            pool_card()
            fused("mc", "offc", c3, RC)
            score("kC", "mc", c3, RC, False, True)
        scan(T.sP[:], T.rst[:], T.kC[:, 0:192], A_.mult, ["rst", "kC"], ["sP"])
        ts(T.lo[:, 0:12], T.sP[:, 15:192:16], 4095, A_.bitwise_and, ["sP"], ["lo"])
        base = "baseR" if back else "baseN"
        ts2(T.loc[:, 0:12], T.lo[:, 0:12], -1.0, T[base][:, 0:1], A_.mult, A_.add, ["lo", base], ["loc"])
        if not last:
            ts(T.sw[:, 0:12], T.lo[:, 0:12], 0.0, A_.is_gt, ["lo"], ["sw"])
            mm(T.pd1[:, 0, 0:12], T.ones[:, 0:128], T.sw[:, 0:12], True, True, ["ones", "sw"], ["pd1"])
            act(T.junk[:, 0:12], T.pd1[:, 0, 0:12], ["pd1"], ["cnt", "junk"], F_.Identity, bias=344.0, accum_out=T.cnt[:])
            act(T.nkt[:], T.cnt[:], ["cnt"], ["nkt"], F_.Identity, scale=-1.0, bias=15.5)
            act(T.K[:], T.cnt[:], ["cnt", "nkt"], ["K"], F_.Identity, bias=T.nkt[:, 0:1])

        def met():
            tt(T.ind[:], T.mc[:].indirect(T.loc[:, 0:12]), T.DA[:], A_.is_ge,
               part("mc", 0, 192) + part("xc", 0, 192) + ["mc_end3072", "mc_end%d" % (MW - 16), "loc", "DA"], ["ind"])
            mm(T.Z[:, 0:192], T.W8[:], T.ind[:], False, False, ["W8", "ind"], ["Z"])
            mm(Dp, T.id4[:], T.ind[:], False, False, ["id4", "ind"], ["Dp"])

        def demands():
            tt(T.tv[:], T.ind[:], nu, A_.mult, ["ind", "Cp"], ["tv"])
            mm(T.Z[:, 0:192], T.W2[:], T.tv[:], False, True, ["W2", "tv"], ["Z"])
            mm(Dp, T.idn[:], T.tv[:], False, True, ["idn", "tv"], ["Dp"])
            if last:
                act(T.ydf[:], Dp, ["Dp"], ["ydf"])
                dma("y", T.yd[:], T.ydf[:], "s_yd", ["ydf"], [])
            else:
                act(T.DA[:], Dp, ["Dp"], ["DA"])

        def change():
            tt(T.tC[:], T.Iw[:].indirect(T.loc[:, 0:12]), T.Q[:], A_.mult,
               ["Iw0", "Iw", "Iw_c0", "Iw_c1", "Iw_end3072", "Iw_end%d" % (MW - 16), "loc", "Q"], ["tC"])

        def spread_change():
            mm(T.pd0[:, 0:12, :], T.BOf[:], T.tC[:], True, True, ["BOf", "tC"], ["pd0"])

        def pack_out():
            tt(X(c_out), T.Cp[:, 0:192], T.tC[:], A_.add, ["Cp", "tC"], [c_out])
            if last:
                dma("s", T.yc[:], X(c_out), "s_yc", [c_out], [])
                return 0
            return send_pack(t)

        def pool_change():
            tt(T.OO[:], T.OHO[:], T.pd0[:, 0:12, :], A_.mult, ["OHO", "pd0"], ["OO"])

        def pool_out():
            out, name = (T.yof[:], "yof") if last else (T.Op[:, 0:192], "Op")
            tt(out, T.Op[:, 0:192], T.OO[:], A_.subtract, ["Op", "OO"], [name])
        if t < 3:
            met()
            change()
            spread_change()
            demands()
            left += pack_out()
            demands_to_dx(2 if t else 1)
            pool_change()
            weave([round_z, make_v] + pool_list, [pool_out] + copies(range(KS + KG, 16), RN))
        elif not last:
            nxt, gone = "cin%d" % (t + 1), "cout%d" % (t - 3)
            change()
            spread_change()
            met()
            left += pack_out()
            demands()
            demands_to_dx(0)
            mm(T.kC[:, 192:384], T.idf[:], X(gone), True, True, ["idf", gone], ["kC"])
            mm(T.pd1[:, 0:12, :], T.nidf[:], X(gone), True, False, ["nidf", gone], ["pd1"])
            pool_change()
            arrived(nxt, "arr%d" % (t + 1), 8)
            mm(T.pd1[:, 0:12, :], T.idf[:], X(nxt), False, True, ["idf", nxt], ["pd1"])
            weave([round_z, make_v] + pool_list,
                  [pool_out, lambda: None, times("mi", T.kC[:, 192:384], "kC"), shift("mf", "mi"),
                   lambda: gather(True, "xo", "offo", XF, 192) if XF < 192 else None,
                   lambda: ts2(T.pd1[:, 0:12, :], T.pd1[:, 0:12, :], 0.0, float(WT), A_.not_equal, A_.mult, ["pd1"], ["pd1"])])
        else:
            met()
            change()
            demands()
            spread_change()
            pack_out()
            pool_change()
            pool_out()
            dma("y", T.yo[:], T.yof[:], "s_yo", ["yof"], [])
    for sem in ("sv", "ss", "sp", "sg"):
        need("g", sem, count[sem])
    for sem in ("l_po", "l_dm", "l_pk", "l_wt", "l_xt", "l_w2", "l_p1", "l_p2", "l_i0", "l_i1", "s_yc", "s_yo", "s_yd"):
        need("g", sem, 16)
    need("g", "l_ph", 128)
    g.wait_ge(T.sem.ls, left)
